import numpy as np
import ml_dtypes


def mxq(x, axis, fmt="e4m3"):
    dtype, down = {"e4m3": (ml_dtypes.float8_e4m3fn, 7), "e5m2": (ml_dtypes.float8_e5m2, 14)}[fmt]
    v = np.moveaxis(np.asarray(x, np.float32).astype(ml_dtypes.bfloat16).astype(np.float64), axis, -1)
    blocks = v.reshape(v.shape[:-1] + (-1, 32))
    amax = np.abs(blocks).max(-1, keepdims=True)
    byte = np.maximum(np.where(amax > 0, np.frexp(amax)[1] - 1 + 127, 0) - down, 1)
    scale = np.exp2(byte - 127.0)
    codes = (blocks / scale).astype(np.float32).astype(dtype).astype(np.float64)
    return np.moveaxis((codes * scale).reshape(v.shape), -1, axis)


WIDE = False


def mx_kscale(k):
    if not WIDE:
        return np.ones(k)
    levels = np.array([10, -10, 5, -5, 0])
    if k % 512:
        return np.exp2(np.random.permutation(np.resize(levels, k // 32))).repeat(32)
    a = np.empty((k // 512, 16))
    for p in range(k // 512):
        a[p, :8] = np.random.permutation(np.resize(levels, 8))
        for g in range(8):
            far = levels[np.abs(levels - a[p, g]) >= 10]
            a[p, g + 8] = far[np.random.randint(len(far))]
    return np.exp2(a.ravel()).repeat(32)


def f64(x):
    return np.asarray(x).astype(np.float64)


def striped(idx):
    return np.tile(idx.reshape(-1, 16).T, (8, 1)).astype(np.uint16)


def unstriped(offs):
    return offs[:16].T.reshape(-1).astype(np.int64)


E2M1 = np.array([0.0, 0.5, 1.0, 1.5, 2.0, 3.0, 4.0, 6.0, -0.0, -0.5, -1.0, -1.5, -2.0, -3.0, -4.0, -6.0])


def pack_fp4(w):
    k, n = w.shape
    w = f64(np.asarray(w, np.float32).astype(ml_dtypes.bfloat16)).reshape(k // 32, 32, n)
    amax = np.abs(w).max(1)
    mant, ex = np.frexp(amax / 6.0)
    byte = np.clip(np.where(amax > 0, np.where(mant > 0.5, ex, ex - 1) + 127, 1), 1, 254)
    scaled = (w * np.exp2(127.0 - byte)[:, None, :]).reshape(k, n).astype(np.float32)
    c = np.ascontiguousarray(scaled.reshape(k // 512, 128, 4, n).transpose(0, 1, 3, 2)).astype(ml_dtypes.float4_e2m1fn).view(np.uint8) & 0xF
    words = (c[..., 0::2] | (c[..., 1::2] << 4)).reshape(k // 512, 128, 2 * n)
    return np.ascontiguousarray(words), np.ascontiguousarray(byte.astype(np.uint8).reshape(k // 512, 16, n))


def unpack_fp4(words, scales):
    g, _, n = scales.shape
    words = np.ascontiguousarray(words).reshape(g, 128, n, 2)
    nib = np.empty((g, 128, n, 4), np.uint8)
    nib[..., 0::2] = words & 0xF
    nib[..., 1::2] = words >> 4
    vals = E2M1[nib] * np.repeat(np.exp2(scales.astype(np.float64) - 127.0), 8, axis=1)[..., None]
    return vals.transpose(0, 1, 3, 2).reshape(g * 512, n)


K, T, S, V, N = 512, 4096, 1024, 512, 256
P = 2 ** 7


def setup_inputs():
    n = np.random.standard_normal
    s = mx_kscale(K)[:, None]
    packed_w1 = pack_fp4(n((K, N)) / np.sqrt(K) / s)
    return {
        "xT": (n((K, T)) * s).astype(np.float32),
        "w1_words": packed_w1[0],
        "w1_scales": packed_w1[1],
        "bound": np.tile(np.random.uniform(0.3, 1.2, V), (P, 1)).astype(np.float32),
        "offs": striped(np.random.permutation(T)[:S]),
        "cen": striped(np.random.permutation(S)[:V]),
        "pos1": striped(np.random.permutation(S)[:V]),
        "pos2": striped(np.random.permutation(S)[:V]),
        "pos3": striped(np.random.permutation(S)[:V]),
    }


def reference(xT, w1_words, w1_scales, bound, offs, cen, pos1, pos2, pos3):
    xq = mxq(f64(xT)[:, unstriped(offs)], 0, "e4m3")
    y = unpack_fp4(w1_words, w1_scales).T @ xq
    yc = y[:, unstriped(cen)]
    low = -1.0 * f64(bound)[:1]
    return yc + (np.maximum(np.minimum(y[:, unstriped(pos1)] - yc, f64(bound)[:1]), low) + np.maximum(np.minimum(y[:, unstriped(pos2)] - yc, f64(bound)[:1]), low) + np.maximum(np.minimum(y[:, unstriped(pos3)] - yc, f64(bound)[:1]), low)) / 3

@@ -1,0 +1,212 @@
+from contextlib import ExitStack
+
+import concourse.mybir as mybir
+from concourse.masks import make_identity
+
+K, T, S, V, N = 512, 4096, 1024, 512, 256
+FLOPS = 2 * K * N * S
+
+F32 = mybir.dt.float32
+BF16 = mybir.dt.bfloat16
+I32 = mybir.dt.int32
+U32 = mybir.dt.uint32
+U16 = mybir.dt.uint16
+U8 = mybir.dt.uint8
+FP8X4 = mybir.dt.float8_e4m3fn_x4
+FP4X4 = mybir.dt.float4_e2m1fn_x4
+ALU = mybir.AluOpType
+COPY = mybir.ActivationFunctionType.Copy
+
+P = 128
+PACK = 4
+HALF = S // 2
+D = 3
+PIECES = {2: [(2048, "scalar"), (2048, "vector")], 3: [(2048, "vector"), (1024, "scalar"), (768, "vector"), (256, "scalar")]}
+UNITS = [(0, 0, 256, "vector"), (0, 256, 256, "vector"), (1, 0, 256, "vector"), (1, 256, 128, "vector"), (1, 384, 128, "direct")]
+LATE = [(256, "scalar"), (256, "vector")]
+
+
+def tile_picked_huber_none_e_kernel(
+    tc, xT, w1_words, w1_scales, bound, offs, cen, pos1, pos2, pos3, out
+):
+    nc = tc.nc
+    with ExitStack() as ctx:
+        keep = ctx.enter_context(tc.tile_pool(name="keep", bufs=1))
+        psum = ctx.enter_context(tc.psum_pool(name="psum", bufs=1))
+
+        rows = xT.rearrange("(p j) t -> p j t", j=PACK)
+        planes = [keep.tile([P, T], F32, name=f"plane{j}") for j in range(PACK)]
+        rounded = {j: keep.tile([P, T], BF16, name=f"rounded{j}") for j in PIECES}
+
+        def load_list(src, name):
+            tile = keep.tile(list(src.shape), U16, name=name)
+            nc.sync.dma_start(tile[:], src)
+            return tile
+
+        w_scales = keep.tile([P, N], U8, name="w_scales", align_bytes=64)
+        nc.vector.memset(w_scales[:].bitcast(I32), 0)
+        bound_rows = keep.tile([P, P], F32, name="bound_rows")
+        nc.vector.memset(bound_rows[:], 0.0)
+        ident = keep.tile([P, P], F32, name="ident")
+        make_identity(nc, ident[:])
+
+        nc.sync.dma_start(planes[0][:], rows[:, 0, :])
+        offs_sb = load_list(offs, "offs_sb")
+        nc.sync.dma_start(planes[1][:], rows[:, 1, :])
+        cen_sb = load_list(cen, "cen_sb")
+        pos_sb = [load_list(src, f"pos{d}_sb") for d, src in enumerate((pos1, pos2, pos3))]
+        w_words = keep.tile([P, 2 * N], U8, name="w_words", align_bytes=64)
+        nc.sync.dma_start(w_words[:], w1_words[0])
+        for q in range(4):
+            nc.sync.dma_start(
+                w_scales[32 * q : 32 * q + 4, :].bitcast(I32),
+                w1_scales[0, 4 * q : 4 * q + 4, :].bitcast(I32),
+            )
+        nc.sync.dma_start(
+            bound_rows[0 : V // P, :], bound[0].rearrange("(c p) -> c p", p=P)
+        )
+
+        bound_t = psum.tile([P, P], F32, name="bound_t")
+        nc.tensor.transpose(bound_t[:], bound_rows[:], ident[:])
+        upper = keep.tile([P, V // P], F32, name="upper")
+        lower = keep.tile([P, V // P], F32, name="lower")
+        nc.scalar.activation(upper[:], bound_t[:, 0 : V // P], COPY)
+        nc.scalar.activation(lower[:], bound_t[:, 0 : V // P], COPY, scale=-1.0)
+
+        upper3 = keep.tile([P, V // P], F32, name="upper3")
+        lower3 = keep.tile([P, V // P], F32, name="lower3")
+        nc.scalar.activation(upper3[:], bound_t[:, 0 : V // P], COPY, scale=1.0 / D)
+        nc.scalar.activation(lower3[:], bound_t[:, 0 : V // P], COPY, scale=-1.0 / D)
+
+        picked = [
+            keep.tile([P, HALF, PACK], BF16, name=f"picked{h}", align_bytes=64)
+            for h in range(2)
+        ]
+        offs_half = [offs_sb[:, h * HALF // 16 : (h + 1) * HALF // 16] for h in range(2)]
+        for j in range(PACK):
+            if j not in PIECES:
+                for h in range(2):
+                    nc.vector.tensor_copy(
+                        picked[h][:, :, j], planes[j][:].indirect(offs_half[h])
+                    )
+                continue
+            start = 0
+            for width, engine in PIECES[j]:
+                cols = slice(start, start + width)
+                nc.sync.dma_start(planes[j][:, cols], rows[:, j, cols])
+                if engine == "vector":
+                    nc.vector.tensor_copy(rounded[j][:, cols], planes[j][:, cols])
+                else:
+                    nc.scalar.copy(rounded[j][:, cols], planes[j][:, cols])
+                start += width
+            nc.vector.tensor_copy(picked[0][:, :, j], planes[j][:].indirect(offs_half[0]))
+            nc.scalar.activation(
+                picked[1][:, :, j], rounded[j][:].indirect(offs_half[1]), COPY
+            )
+
+        codes = [keep.tile([P, HALF], U32, name=f"codes{h}", align_bytes=64) for h in range(2)]
+        scales = [keep.tile([P, HALF], U8, name=f"scales{h}", align_bytes=64) for h in range(2)]
+
+        def quantize(h, cols):
+            nc.vector.quantize_mx(
+                out=codes[h][:, cols].bitcast(FP8X4),
+                scales=scales[h][:, cols],
+                in_=picked[h][:, cols, :].rearrange("p n j -> p (n j)"),
+            )
+
+        y = [keep.tile([P, S], F32, name=f"y{b}") for b in range(N // P)]
+
+        def project(b, h, cols, tag, bufs, engine):
+            width = cols.stop - cols.start
+            acc = psum.tile([P, width], F32, name="acc", tag=tag, bufs=bufs)
+            nc.tensor.matmul_mx(
+                out=acc[:],
+                lhsT=w_words[:, 2 * P * b : 2 * P * (b + 1)].bitcast(FP4X4),
+                lhsT_scale=w_scales[:, P * b : P * (b + 1)],
+                rhs=codes[h][:, cols].bitcast(FP8X4),
+                rhs_scale=scales[h][:, cols],
+                start=True,
+                stop=True,
+            )
+            copy_out(engine, y[b][:, h * HALF + cols.start : h * HALF + cols.stop], acc[:])
+
+        def copy_out(engine, dst, src):
+            if engine == "vector":
+                nc.vector.tensor_copy(dst, src)
+            else:
+                nc.scalar.copy(dst, src)
+
+        quantize(0, slice(0, HALF))
+        project(0, 0, slice(0, HALF), "pull", 5, "scalar")
+        start = 0
+        for width, engine in LATE:
+            cols = slice(start, start + width)
+            quantize(1, cols)
+            project(0, 1, cols, "pull", 5, engine)
+            start += width
+        for h in range(2):
+            project(1, h, slice(0, HALF), "total", 2, "scalar")
+
+        def chunk_of(tile, c):
+            return tile[:, c * P : (c + 1) * P]
+
+        for u, (b, v0, width, mode) in enumerate(UNITS):
+            chunks = width // P
+            direct = mode == "direct"
+            entries = slice(v0 // 16, (v0 + width) // 16)
+            centre = keep.tile([P, width], F32, name=f"centre{u}")
+            nc.vector.tensor_copy(centre[:], y[b][:].indirect(cen_sb[:, entries]))
+            slots = D if direct else D + 1
+            pulls = [
+                psum.tile([P, slots * P], F32, name="pull", tag="pull", bufs=5)
+                for c in range(chunks)
+            ]
+            if not direct:
+                for c in range(chunks):
+                    nc.tensor.matmul(
+                        chunk_of(pulls[c], D), chunk_of(centre, c), ident[:],
+                        start=True, stop=False, is_transpose=True,
+                    )
+            for d in range(D):
+                near = keep.tile([P, width], F32, name="near", tag="near", bufs=3)
+                window = y[b][:].indirect(pos_sb[d][:, entries])
+                nc.vector.tensor_tensor(near[:], window, centre[:], ALU.subtract)
+                for c in range(chunks):
+                    nc.tensor.matmul(
+                        chunk_of(pulls[c], d), chunk_of(near, c), ident[:],
+                        start=(direct and d == 0), stop=(d == D - 1), is_transpose=True,
+                    )
+            total = psum.tile([P, width], F32, name="total", tag="total", bufs=2)
+            for c in range(chunks):
+                col = slice(v0 // P + c, v0 // P + c + 1)
+                clipped = keep.tile([P, D * P], F32, name=f"clipped{u}_{c}")
+                terms = [chunk_of(clipped, d) for d in range(D)]
+                if direct:
+                    nc.vector.tensor_scalar(
+                        clipped[:], pulls[c][:], upper[:, col], lower[:, col], ALU.min, ALU.max
+                    )
+                else:
+                    raw = keep.tile([P, D * P], F32, name=f"raw{u}_{c}")
+                    nc.scalar.activation(raw[:], pulls[c][:, 0 : D * P], COPY, scale=1.0 / D)
+                    turned = keep.tile([P, P], F32, name=f"turned{u}_{c}")
+                    nc.scalar.copy(turned[:], chunk_of(pulls[c], D))
+                    terms = [turned[:]] + terms
+                    engine = nc.vector if mode == "vector" else nc.gpsimd
+                    engine.tensor_scalar(
+                        clipped[:], raw[:], upper3[:, col], lower3[:, col], ALU.min, ALU.max
+                    )
+                for i, term in enumerate(terms):
+                    nc.tensor.matmul(
+                        chunk_of(total, c), term, ident[:],
+                        start=(c == 0 and i == 0),
+                        stop=(c == chunks - 1 and i == len(terms) - 1),
+                        is_transpose=True,
+                    )
+            result = keep.tile([P, width], F32, name=f"result{u}")
+            if direct:
+                nc.vector.scalar_tensor_tensor(
+                    result[:], total[:], 1.0 / D, centre[:], ALU.mult, ALU.add
+                )
+            else:
+                nc.scalar.copy(result[:], total[:])
+            nc.sync.dma_start(out[b * P : (b + 1) * P, v0 : v0 + width], result[:])

@@ -19,11 +19,32 @@ COPY = mybir.ActivationFunctionType.Copy
 
 P = 128
 PACK = 4
+LAST = PACK - 1
 HALF = S // 2
 D = 3
-PIECES = {2: [(2048, "scalar"), (2048, "vector")], 3: [(2048, "vector"), (1024, "scalar"), (768, "vector"), (256, "scalar")]}
-UNITS = [(0, 0, 256, "vector"), (0, 256, 256, "vector"), (1, 0, 256, "vector"), (1, 256, 128, "vector"), (1, 384, 128, "direct")]
-LATE = [(256, "scalar"), (256, "vector")]
+PER_COLUMN = 16
+QUADRANT = 32
+
+LAST_PIECES = [
+    (1024, "scalar"),
+    (1024, "scalar"),
+    (1024, "scalar"),
+    (640, "vector"),
+    (256, "vector"),
+    (128, "vector"),
+]
+FIRST_BLOCK_STEPS = [
+    (0, 0, 256, "scalar"),
+    (0, 256, 256, "scalar"),
+    (1, 0, 256, "vector"),
+    (1, 256, 128, "scalar"),
+    (1, 384, 128, "vector"),
+]
+SECOND_BLOCK_BANK = len(FIRST_BLOCK_STEPS) - 2
+BOUND_BANK = 7
+BANK_TURN = [0, 1, 2, 5, 6, 7, 3, 4]
+UNIT = 256
+PULL_BUFS = 4
 
 
 def tile_picked_huber_none_e_kernel(
@@ -34,14 +55,25 @@ def tile_picked_huber_none_e_kernel(
         keep = ctx.enter_context(tc.tile_pool(name="keep", bufs=1))
         psum = ctx.enter_context(tc.psum_pool(name="psum", bufs=1))
 
-        rows = xT.rearrange("(p j) t -> p j t", j=PACK)
-        planes = [keep.tile([P, T], F32, name=f"plane{j}") for j in range(PACK)]
-        rounded = {j: keep.tile([P, T], BF16, name=f"rounded{j}") for j in PIECES}
-
         def load_list(src, name):
             tile = keep.tile(list(src.shape), U16, name=name)
             nc.sync.dma_start(tile[:], src)
             return tile
+
+        def entries(list_tile, first, count):
+            return list_tile[:, first // PER_COLUMN : (first + count) // PER_COLUMN]
+
+        def copy_on(engine, dst, src):
+            if engine == "vector":
+                nc.vector.tensor_copy(dst, src)
+            else:
+                nc.scalar.copy(dst, src)
+
+        def bank_tile(width, name, bank):
+            return psum.tile([P, width], F32, name=name, tag=f"bank{bank}")
+
+        def part(tile, i):
+            return tile[:, i * P : (i + 1) * P]
 
         w_scales = keep.tile([P, N], U8, name="w_scales", align_bytes=64)
         nc.vector.memset(w_scales[:].bitcast(I32), 0)
@@ -50,163 +82,124 @@ def tile_picked_huber_none_e_kernel(
         ident = keep.tile([P, P], F32, name="ident")
         make_identity(nc, ident[:])
 
+        rows = xT.rearrange("(p t) c -> p t c", t=PACK)
+        planes = [keep.tile([P, T], F32, name=f"plane{t}") for t in range(PACK)]
         nc.sync.dma_start(planes[0][:], rows[:, 0, :])
         offs_sb = load_list(offs, "offs_sb")
-        nc.sync.dma_start(planes[1][:], rows[:, 1, :])
-        cen_sb = load_list(cen, "cen_sb")
-        pos_sb = [load_list(src, f"pos{d}_sb") for d, src in enumerate((pos1, pos2, pos3))]
         w_words = keep.tile([P, 2 * N], U8, name="w_words", align_bytes=64)
         nc.sync.dma_start(w_words[:], w1_words[0])
-        for q in range(4):
+        cen_sb = load_list(cen, "cen_sb")
+        pos_sb = [load_list(src, f"pos{d}_sb") for d, src in enumerate((pos1, pos2, pos3))]
+        for t in range(1, LAST):
+            nc.sync.dma_start(planes[t][:], rows[:, t, :])
+        for q in range(P // QUADRANT):
             nc.sync.dma_start(
-                w_scales[32 * q : 32 * q + 4, :].bitcast(I32),
+                w_scales[QUADRANT * q : QUADRANT * q + 4, :].bitcast(I32),
                 w1_scales[0, 4 * q : 4 * q + 4, :].bitcast(I32),
             )
-        nc.sync.dma_start(
-            bound_rows[0 : V // P, :], bound[0].rearrange("(c p) -> c p", p=P)
-        )
+        nc.sync.dma_start(bound_rows[0 : V // P, :], bound[0].rearrange("(c p) -> c p", p=P))
+        pieces = []
+        first = 0
+        for width, engine in LAST_PIECES:
+            cols = slice(first, first + width)
+            nc.sync.dma_start(planes[LAST][:, cols], rows[:, LAST, cols])
+            pieces.append((cols, engine))
+            first += width
 
-        bound_t = psum.tile([P, P], F32, name="bound_t")
+        bound_t = bank_tile(P, "bound_t", BOUND_BANK)
         nc.tensor.transpose(bound_t[:], bound_rows[:], ident[:])
         upper = keep.tile([P, V // P], F32, name="upper")
         lower = keep.tile([P, V // P], F32, name="lower")
-        nc.scalar.activation(upper[:], bound_t[:, 0 : V // P], COPY)
+        nc.scalar.activation(upper[:], bound_t[:, 0 : V // P], COPY, scale=1.0)
         nc.scalar.activation(lower[:], bound_t[:, 0 : V // P], COPY, scale=-1.0)
 
-        upper3 = keep.tile([P, V // P], F32, name="upper3")
-        lower3 = keep.tile([P, V // P], F32, name="lower3")
-        nc.scalar.activation(upper3[:], bound_t[:, 0 : V // P], COPY, scale=1.0 / D)
-        nc.scalar.activation(lower3[:], bound_t[:, 0 : V // P], COPY, scale=-1.0 / D)
-
         picked = [
-            keep.tile([P, HALF, PACK], BF16, name=f"picked{h}", align_bytes=64)
-            for h in range(2)
+            keep.tile([P, HALF, PACK], BF16, name=f"picked{h}", align_bytes=64) for h in range(2)
         ]
-        offs_half = [offs_sb[:, h * HALF // 16 : (h + 1) * HALF // 16] for h in range(2)]
-        for j in range(PACK):
-            if j not in PIECES:
-                for h in range(2):
-                    nc.vector.tensor_copy(
-                        picked[h][:, :, j], planes[j][:].indirect(offs_half[h])
-                    )
-                continue
-            start = 0
-            for width, engine in PIECES[j]:
-                cols = slice(start, start + width)
-                nc.sync.dma_start(planes[j][:, cols], rows[:, j, cols])
-                if engine == "vector":
-                    nc.vector.tensor_copy(rounded[j][:, cols], planes[j][:, cols])
-                else:
-                    nc.scalar.copy(rounded[j][:, cols], planes[j][:, cols])
-                start += width
-            nc.vector.tensor_copy(picked[0][:, :, j], planes[j][:].indirect(offs_half[0]))
-            nc.scalar.activation(
-                picked[1][:, :, j], rounded[j][:].indirect(offs_half[1]), COPY
-            )
+        halves = [entries(offs_sb, h * HALF, HALF) for h in range(2)]
+        for t in range(LAST):
+            for h in range(2):
+                nc.vector.tensor_copy(picked[h][:, :, t], planes[t][:].indirect(halves[h]))
+        rounded = keep.tile([P, T], BF16, name="rounded")
+        for cols, engine in pieces:
+            copy_on(engine, rounded[:, cols], planes[LAST][:, cols])
+        nc.vector.tensor_copy(picked[0][:, :, LAST], planes[LAST][:].indirect(halves[0]))
+        nc.scalar.activation(picked[1][:, :, LAST], rounded[:].indirect(halves[1]), COPY)
 
         codes = [keep.tile([P, HALF], U32, name=f"codes{h}", align_bytes=64) for h in range(2)]
         scales = [keep.tile([P, HALF], U8, name=f"scales{h}", align_bytes=64) for h in range(2)]
-
-        def quantize(h, cols):
-            nc.vector.quantize_mx(
-                out=codes[h][:, cols].bitcast(FP8X4),
-                scales=scales[h][:, cols],
-                in_=picked[h][:, cols, :].rearrange("p n j -> p (n j)"),
-            )
-
         y = [keep.tile([P, S], F32, name=f"y{b}") for b in range(N // P)]
 
-        def project(b, h, cols, tag, bufs, engine):
-            width = cols.stop - cols.start
-            acc = psum.tile([P, width], F32, name="acc", tag=tag, bufs=bufs)
+        def project(b, h, cols, bank, engine):
+            acc = bank_tile(cols.stop - cols.start, "acc", bank)
             nc.tensor.matmul_mx(
                 out=acc[:],
                 lhsT=w_words[:, 2 * P * b : 2 * P * (b + 1)].bitcast(FP4X4),
-                lhsT_scale=w_scales[:, P * b : P * (b + 1)],
+                lhsT_scale=part(w_scales, b),
                 rhs=codes[h][:, cols].bitcast(FP8X4),
                 rhs_scale=scales[h][:, cols],
                 start=True,
                 stop=True,
             )
-            copy_out(engine, y[b][:, h * HALF + cols.start : h * HALF + cols.stop], acc[:])
+            copy_on(engine, y[b][:, h * HALF + cols.start : h * HALF + cols.stop], acc[:])
 
-        def copy_out(engine, dst, src):
-            if engine == "vector":
-                nc.vector.tensor_copy(dst, src)
-            else:
-                nc.scalar.copy(dst, src)
-
-        quantize(0, slice(0, HALF))
-        project(0, 0, slice(0, HALF), "pull", 5, "scalar")
-        start = 0
-        for width, engine in LATE:
-            cols = slice(start, start + width)
-            quantize(1, cols)
-            project(0, 1, cols, "pull", 5, engine)
-            start += width
+        for bank, (h, first, width, engine) in enumerate(FIRST_BLOCK_STEPS):
+            cols = slice(first, first + width)
+            nc.vector.quantize_mx(
+                out=codes[h][:, cols].bitcast(FP8X4),
+                scales=scales[h][:, cols],
+                in_=picked[h][:, cols, :].rearrange("p j t -> p (j t)"),
+            )
+            project(0, h, cols, bank, engine)
         for h in range(2):
-            project(1, h, slice(0, HALF), "total", 2, "scalar")
+            project(1, h, slice(0, HALF), SECOND_BLOCK_BANK + h, "scalar")
 
-        def chunk_of(tile, c):
-            return tile[:, c * P : (c + 1) * P]
+        def turn(dst, src, start, stop):
+            nc.tensor.matmul(dst, src, ident[:], start=start, stop=stop, is_transpose=True)
 
-        for u, (b, v0, width, mode) in enumerate(UNITS):
-            chunks = width // P
-            direct = mode == "direct"
-            entries = slice(v0 // 16, (v0 + width) // 16)
-            centre = keep.tile([P, width], F32, name=f"centre{u}")
-            nc.vector.tensor_copy(centre[:], y[b][:].indirect(cen_sb[:, entries]))
-            slots = D if direct else D + 1
-            pulls = [
-                psum.tile([P, slots * P], F32, name="pull", tag="pull", bufs=5)
-                for c in range(chunks)
-            ]
-            if not direct:
-                for c in range(chunks):
-                    nc.tensor.matmul(
-                        chunk_of(pulls[c], D), chunk_of(centre, c), ident[:],
-                        start=True, stop=False, is_transpose=True,
-                    )
+        units = [(b, v0) for b in range(N // P) for v0 in range(0, V, UNIT)]
+        chunks = UNIT // P
+        banks = BANK_TURN * 2
+        for u, (b, v0) in enumerate(units):
+            final = u == len(units) - 1
+            centre = keep.tile([P, UNIT], F32, name=f"centre{u}")
+            nc.vector.tensor_copy(centre[:], y[b][:].indirect(entries(cen_sb, v0, UNIT)))
+
+            turned = [bank_tile(D * P, "turned", banks.pop(0)) for c in range(chunks)]
             for d in range(D):
-                near = keep.tile([P, width], F32, name="near", tag="near", bufs=3)
-                window = y[b][:].indirect(pos_sb[d][:, entries])
-                nc.vector.tensor_tensor(near[:], window, centre[:], ALU.subtract)
-                for c in range(chunks):
-                    nc.tensor.matmul(
-                        chunk_of(pulls[c], d), chunk_of(near, c), ident[:],
-                        start=(direct and d == 0), stop=(d == D - 1), is_transpose=True,
-                    )
-            total = psum.tile([P, width], F32, name="total", tag="total", bufs=2)
-            for c in range(chunks):
-                col = slice(v0 // P + c, v0 // P + c + 1)
-                clipped = keep.tile([P, D * P], F32, name=f"clipped{u}_{c}")
-                terms = [chunk_of(clipped, d) for d in range(D)]
-                if direct:
-                    nc.vector.tensor_scalar(
-                        clipped[:], pulls[c][:], upper[:, col], lower[:, col], ALU.min, ALU.max
-                    )
-                else:
-                    raw = keep.tile([P, D * P], F32, name=f"raw{u}_{c}")
-                    nc.scalar.activation(raw[:], pulls[c][:, 0 : D * P], COPY, scale=1.0 / D)
-                    turned = keep.tile([P, P], F32, name=f"turned{u}_{c}")
-                    nc.scalar.copy(turned[:], chunk_of(pulls[c], D))
-                    terms = [turned[:]] + terms
-                    engine = nc.vector if mode == "vector" else nc.gpsimd
-                    engine.tensor_scalar(
-                        clipped[:], raw[:], upper3[:, col], lower3[:, col], ALU.min, ALU.max
-                    )
-                for i, term in enumerate(terms):
-                    nc.tensor.matmul(
-                        chunk_of(total, c), term, ident[:],
-                        start=(c == 0 and i == 0),
-                        stop=(c == chunks - 1 and i == len(terms) - 1),
-                        is_transpose=True,
-                    )
-            result = keep.tile([P, width], F32, name=f"result{u}")
-            if direct:
-                nc.vector.scalar_tensor_tensor(
-                    result[:], total[:], 1.0 / D, centre[:], ALU.mult, ALU.add
+                pull = keep.tile([P, UNIT], F32, name="pull", tag="pull", bufs=PULL_BUFS)
+                nc.vector.tensor_tensor(
+                    pull[:], y[b][:].indirect(entries(pos_sb[d], v0, UNIT)), centre[:], ALU.subtract
                 )
-            else:
-                nc.scalar.copy(result[:], total[:])
-            nc.sync.dma_start(out[b * P : (b + 1) * P, v0 : v0 + width], result[:])
+                for c in range(chunks):
+                    turn(part(turned[c], d), part(pull, c), d == 0, d == D - 1)
+
+            group = 1 if final else chunks
+            for c0 in range(0, chunks, group):
+                total = bank_tile(group * P, "total", banks.pop(0))
+                for c in range(c0, c0 + group):
+                    if final:
+                        source = turned[c]
+                    else:
+                        source = keep.tile([P, D * P], F32, name=f"source{u}_{c}")
+                        nc.scalar.activation(source[:], turned[c][:], COPY, scale=1.0)
+                    col = slice(v0 // P + c, v0 // P + c + 1)
+                    clipped = keep.tile([P, D * P], F32, name=f"clipped{u}_{c}")
+                    nc.vector.tensor_scalar(
+                        clipped[:], source[:], upper[:, col], lower[:, col], ALU.min, ALU.max
+                    )
+                    for d in range(D):
+                        turn(
+                            part(total, c - c0),
+                            part(clipped, d),
+                            c == c0 and d == 0,
+                            c == c0 + group - 1 and d == D - 1,
+                        )
+                span = slice(c0 * P, (c0 + group) * P)
+                result = keep.tile([P, group * P], F32, name=f"result{u}_{c0}")
+                nc.vector.scalar_tensor_tensor(
+                    result[:], total[:], 1.0 / D, centre[:, span], ALU.mult, ALU.add
+                )
+                nc.sync.dma_start(
+                    out[b * P : (b + 1) * P, v0 + span.start : v0 + span.stop], result[:]
+                )

@@ -86,18 +86,9 @@ def tile_picked_huber_none_e_kernel(
         planes = [keep.tile([P, T], F32, name=f"plane{t}") for t in range(PACK)]
         nc.sync.dma_start(planes[0][:], rows[:, 0, :])
         offs_sb = load_list(offs, "offs_sb")
-        w_words = keep.tile([P, 2 * N], U8, name="w_words", align_bytes=64)
-        nc.sync.dma_start(w_words[:], w1_words[0])
-        cen_sb = load_list(cen, "cen_sb")
-        pos_sb = [load_list(src, f"pos{d}_sb") for d, src in enumerate((pos1, pos2, pos3))]
+        nc.sync.dma_start(bound_rows[0 : V // P, :], bound[0].rearrange("(c p) -> c p", p=P))
         for t in range(1, LAST):
             nc.sync.dma_start(planes[t][:], rows[:, t, :])
-        for q in range(P // QUADRANT):
-            nc.sync.dma_start(
-                w_scales[QUADRANT * q : QUADRANT * q + 4, :].bitcast(I32),
-                w1_scales[0, 4 * q : 4 * q + 4, :].bitcast(I32),
-            )
-        nc.sync.dma_start(bound_rows[0 : V // P, :], bound[0].rearrange("(c p) -> c p", p=P))
         pieces = []
         first = 0
         for width, engine in LAST_PIECES:
@@ -105,6 +96,15 @@ def tile_picked_huber_none_e_kernel(
             nc.sync.dma_start(planes[LAST][:, cols], rows[:, LAST, cols])
             pieces.append((cols, engine))
             first += width
+        w_words = keep.tile([P, 2 * N], U8, name="w_words", align_bytes=64)
+        nc.sync.dma_start(w_words[:], w1_words[0])
+        for q in range(P // QUADRANT):
+            nc.sync.dma_start(
+                w_scales[QUADRANT * q : QUADRANT * q + 4, :].bitcast(I32),
+                w1_scales[0, 4 * q : 4 * q + 4, :].bitcast(I32),
+            )
+        cen_sb = load_list(cen, "cen_sb")
+        pos_sb = [load_list(src, f"pos{d}_sb") for d, src in enumerate((pos1, pos2, pos3))]
 
         bound_t = bank_tile(P, "bound_t", BOUND_BANK)
         nc.tensor.transpose(bound_t[:], bound_rows[:], ident[:])

@@ -42,7 +42,10 @@ FIRST_BLOCK_STEPS = [
 ]
 SECOND_BLOCK_BANK = len(FIRST_BLOCK_STEPS) - 2
 BOUND_BANK = 7
-BANK_TURN = [0, 1, 2, 5, 6, 7, 3, 4]
+TURNED_BANKS = [(0, 1), (2, 5)]
+TOTAL_BANKS = [6, 7]
+LATE_BANK = 3
+LAST_BANKS = [4, 0]
 UNIT = 256
 PULL_BUFS = 4
 
@@ -159,47 +162,99 @@ def tile_picked_huber_none_e_kernel(
 
         units = [(b, v0) for b in range(N // P) for v0 in range(0, V, UNIT)]
         chunks = UNIT // P
-        banks = BANK_TURN * 2
-        for u, (b, v0) in enumerate(units):
-            final = u == len(units) - 1
-            centre = keep.tile([P, UNIT], F32, name=f"centre{u}")
-            nc.vector.tensor_copy(centre[:], y[b][:].indirect(entries(cen_sb, v0, UNIT)))
+        last = len(units) - 1
+        centre, turned, total = {}, {}, {}
 
-            turned = [bank_tile(D * P, "turned", banks.pop(0)) for c in range(chunks)]
-            for d in range(D):
-                pull = keep.tile([P, UNIT], F32, name="pull", tag="pull", bufs=PULL_BUFS)
-                nc.vector.tensor_tensor(
-                    pull[:], y[b][:].indirect(entries(pos_sb[d], v0, UNIT)), centre[:], ALU.subtract
-                )
-                for c in range(chunks):
-                    turn(part(turned[c], d), part(pull, c), d == 0, d == D - 1)
+        def gather_centre(u):
+            b, v0 = units[u]
+            centre[u] = keep.tile([P, UNIT], F32, name=f"centre{u}")
+            nc.vector.tensor_copy(centre[u][:], y[b][:].indirect(entries(cen_sb, v0, UNIT)))
 
-            group = 1 if final else chunks
-            for c0 in range(0, chunks, group):
-                total = bank_tile(group * P, "total", banks.pop(0))
-                for c in range(c0, c0 + group):
-                    if final:
-                        source = turned[c]
-                    else:
-                        source = keep.tile([P, D * P], F32, name=f"source{u}_{c}")
-                        nc.scalar.activation(source[:], turned[c][:], COPY, scale=1.0)
-                    col = slice(v0 // P + c, v0 // P + c + 1)
-                    clipped = keep.tile([P, D * P], F32, name=f"clipped{u}_{c}")
-                    nc.vector.tensor_scalar(
-                        clipped[:], source[:], upper[:, col], lower[:, col], ALU.min, ALU.max
+        def gather_pull(u, d, places, start, stop, tag="pull", bufs=PULL_BUFS):
+            b, v0 = units[u]
+            pull = keep.tile([P, UNIT], F32, name="pull", tag=tag, bufs=bufs)
+            nc.vector.tensor_tensor(
+                pull[:], y[b][:].indirect(entries(pos_sb[d], v0, UNIT)), centre[u][:], ALU.subtract
+            )
+            for c in range(chunks):
+                turn(places[c], part(pull, c), start[c], stop[c])
+
+        def pull_into_turned(u, d, count=D, **kw):
+            if d == 0:
+                turned[u] = [
+                    bank_tile(count * P, "turned", TURNED_BANKS[u % 2][c]) for c in range(chunks)
+                ]
+            gather_pull(
+                u, d, [part(t, d) for t in turned[u]], [d == 0] * chunks, [d == count - 1] * chunks, **kw
+            )
+
+        def clip(u, c, source, name):
+            col = slice(units[u][1] // P + c, units[u][1] // P + c + 1)
+            clipped = keep.tile(list(source.shape), F32, name=name)
+            nc.vector.tensor_scalar(
+                clipped[:], source, upper[:, col], lower[:, col], ALU.min, ALU.max
+            )
+            return clipped
+
+        def empty(u, c):
+            source = keep.tile(list(turned[u][c].shape), F32, name=f"source{u}_{c}")
+            nc.scalar.activation(source[:], turned[u][c][:], COPY, scale=1.0)
+            return source
+
+        def clip_unit(u):
+            total[u] = bank_tile(UNIT, "total", TOTAL_BANKS[u % 2])
+            for c in range(chunks):
+                clipped = clip(u, c, empty(u, c)[:], f"clipped{u}_{c}")
+                for d in range(D):
+                    turn(
+                        part(total[u], c),
+                        part(clipped, d),
+                        c == 0 and d == 0,
+                        c == chunks - 1 and d == D - 1,
                     )
-                    for d in range(D):
-                        turn(
-                            part(total, c - c0),
-                            part(clipped, d),
-                            c == c0 and d == 0,
-                            c == c0 + group - 1 and d == D - 1,
-                        )
-                span = slice(c0 * P, (c0 + group) * P)
-                result = keep.tile([P, group * P], F32, name=f"result{u}_{c0}")
-                nc.vector.scalar_tensor_tensor(
-                    result[:], total[:], 1.0 / D, centre[:, span], ALU.mult, ALU.add
-                )
-                nc.sync.dma_start(
-                    out[b * P : (b + 1) * P, v0 + span.start : v0 + span.stop], result[:]
-                )
+
+        def finish(u, sums, first, width):
+            b, v0 = units[u]
+            result = keep.tile([P, width], F32, name=f"result{u}_{first}")
+            nc.vector.scalar_tensor_tensor(
+                result[:], sums, 1.0 / D, centre[u][:, first : first + width], ALU.mult, ALU.add
+            )
+            nc.sync.dma_start(
+                out[b * P : (b + 1) * P, v0 + first : v0 + first + width], result[:]
+            )
+
+        gather_centre(0)
+        gather_centre(1)
+        for d in range(D):
+            pull_into_turned(0, d)
+        pull_into_turned(1, 0)
+        pull_into_turned(1, 1)
+        gather_centre(2)
+        clip_unit(0)
+        pull_into_turned(1, 2)
+        pull_into_turned(2, 0)
+        pull_into_turned(2, 1)
+        finish(0, total[0][:], 0, UNIT)
+        clip_unit(1)
+        gather_centre(3)
+        pull_into_turned(2, 2)
+        pull_into_turned(3, 0, count=D - 1)
+        finish(1, total[1][:], 0, UNIT)
+        pull_into_turned(3, 1, count=D - 1)
+        clip_unit(2)
+        late = bank_tile(UNIT, "late", LATE_BANK)
+        gather_pull(
+            last, D - 1, [part(late, c) for c in range(chunks)], [True, False], [False, True],
+            tag="source2_0", bufs=1,
+        )
+        sums = [bank_tile(P, "sums", LAST_BANKS[c]) for c in range(chunks)]
+        for c in range(chunks):
+            clipped = clip(last, c, empty(last, c)[:], f"early{c}")
+            for d in range(D - 1):
+                turn(sums[c][:], part(clipped, d), d == 0, False)
+        finish(2, total[2][:], 0, UNIT)
+        for c in range(chunks):
+            clipped = clip(last, c, part(late, c), f"late{c}")
+            turn(sums[c][:], clipped[:], False, True)
+        for c in range(chunks):
+            finish(last, sums[c][:], c * P, P)

@@ -47,7 +47,6 @@ TOTAL_BANKS = [6, 7]
 LATE_BANK = 3
 LAST_BANKS = [4, 0]
 UNIT = 256
-PULL_BUFS = 4
 
 
 def tile_picked_huber_none_e_kernel(
@@ -102,7 +101,7 @@ def tile_picked_huber_none_e_kernel(
         w_words = keep.tile([P, 2 * N], U8, name="w_words", align_bytes=64)
         nc.sync.dma_start(w_words[:], w1_words[0])
         for q in range(P // QUADRANT):
-            nc.sync.dma_start(
+            nc.gpsimd.dma_start(
                 w_scales[QUADRANT * q : QUADRANT * q + 4, :].bitcast(I32),
                 w1_scales[0, 4 * q : 4 * q + 4, :].bitcast(I32),
             )
@@ -165,16 +164,17 @@ def tile_picked_huber_none_e_kernel(
         last = len(units) - 1
         centre, turned, total = {}, {}, {}
 
-        def gather_centre(u):
+        def gather_centre(u, tag=None):
             b, v0 = units[u]
-            centre[u] = keep.tile([P, UNIT], F32, name=f"centre{u}")
+            centre[u] = keep.tile([P, UNIT], F32, name=f"centre{u}", tag=tag or f"centre{u}")
             nc.vector.tensor_copy(centre[u][:], y[b][:].indirect(entries(cen_sb, v0, UNIT)))
 
-        def gather_pull(u, d, places, start, stop, tag="pull", bufs=PULL_BUFS):
+        def gather_pull(u, d, places, start, stop, tag=None, pull=None):
             b, v0 = units[u]
-            pull = keep.tile([P, UNIT], F32, name="pull", tag=tag, bufs=bufs)
+            if pull is None:
+                pull = keep.tile([P, UNIT], F32, name=f"pull{u}_{d}", tag=tag or f"pull{u}_{d}")[:]
             nc.vector.tensor_tensor(
-                pull[:], y[b][:].indirect(entries(pos_sb[d], v0, UNIT)), centre[u][:], ALU.subtract
+                pull, y[b][:].indirect(entries(pos_sb[d], v0, UNIT)), centre[u][:], ALU.subtract
             )
             for c in range(chunks):
                 turn(places[c], part(pull, c), start[c], stop[c])
@@ -190,8 +190,10 @@ def tile_picked_huber_none_e_kernel(
 
         def clip(u, c, source, name):
             col = slice(units[u][1] // P + c, units[u][1] // P + c + 1)
-            clipped = keep.tile(list(source.shape), F32, name=name)
-            nc.vector.tensor_scalar(
+            tag = "source0_1" if (u, c) == (1, 1) else name
+            clipped = keep.tile(list(source.shape), F32, name=name, tag=tag)
+            engine = nc.gpsimd if u == 0 else nc.vector
+            engine.tensor_scalar(
                 clipped[:], source, upper[:, col], lower[:, col], ALU.min, ALU.max
             )
             return clipped
@@ -229,23 +231,25 @@ def tile_picked_huber_none_e_kernel(
             pull_into_turned(0, d)
         pull_into_turned(1, 0)
         pull_into_turned(1, 1)
-        gather_centre(2)
-        clip_unit(0)
         pull_into_turned(1, 2)
-        pull_into_turned(2, 0)
-        pull_into_turned(2, 1)
+        gather_centre(2)
+        gather_centre(3)
+        clip_unit(0)
+        pair = keep.tile([P, 2 * UNIT], F32, name="pair0", tag="source0_1")
+        pull_into_turned(2, 0, pull=pair[:, 0:UNIT])
+        pull_into_turned(2, 1, pull=pair[:, UNIT : 2 * UNIT])
         finish(0, total[0][:], 0, UNIT)
         clip_unit(1)
-        gather_centre(3)
-        pull_into_turned(2, 2)
-        pull_into_turned(3, 0, count=D - 1)
+        pair = keep.tile([P, 2 * UNIT], F32, name="pair1", tag="centre0")
+        pull_into_turned(2, 2, pull=pair[:, 0:UNIT])
+        pull_into_turned(3, 0, count=D - 1, pull=pair[:, UNIT : 2 * UNIT])
+        pull_into_turned(3, 1, count=D - 1, tag="source1_1")
         finish(1, total[1][:], 0, UNIT)
-        pull_into_turned(3, 1, count=D - 1)
         clip_unit(2)
         late = bank_tile(UNIT, "late", LATE_BANK)
         gather_pull(
             last, D - 1, [part(late, c) for c in range(chunks)], [True, False], [False, True],
-            tag="source2_0", bufs=1,
+            tag="source2_0",
         )
         sums = [bank_tile(P, "sums", LAST_BANKS[c]) for c in range(chunks)]
         for c in range(chunks):

@@ -44,8 +44,8 @@ SECOND_BLOCK_BANK = len(FIRST_BLOCK_STEPS) - 2
 BOUND_BANK = 7
 TURNED_BANKS = [(0, 1), (2, 5)]
 TOTAL_BANKS = [6, 7]
-LATE_BANK = 3
-LAST_BANKS = [4, 0]
+LATE_BANKS = [3, 4]
+LAST_BANKS = [0, 1]
 UNIT = 256
 
 
@@ -164,53 +164,49 @@ def tile_picked_huber_none_e_kernel(
         last = len(units) - 1
         centre, turned, total = {}, {}, {}
 
-        def gather_centre(u, tag=None):
-            b, v0 = units[u]
-            centre[u] = keep.tile([P, UNIT], F32, name=f"centre{u}", tag=tag or f"centre{u}")
-            nc.vector.tensor_copy(centre[u][:], y[b][:].indirect(entries(cen_sb, v0, UNIT)))
+        def tile_after(name, width, tag=None):
+            return keep.tile([P, width], F32, name=name, tag=tag or name)[:]
 
-        def gather_pull(u, d, places, start, stop, tag=None, pull=None):
+        def gather_centre(u):
             b, v0 = units[u]
-            if pull is None:
-                pull = keep.tile([P, UNIT], F32, name=f"pull{u}_{d}", tag=tag or f"pull{u}_{d}")[:]
+            centre[u] = tile_after(f"centre{u}", UNIT)
+            nc.vector.tensor_copy(centre[u], y[b][:].indirect(entries(cen_sb, v0, UNIT)))
+
+        def gather_pull(u, d, pull, first, width):
+            b, v0 = units[u]
             nc.vector.tensor_tensor(
-                pull, y[b][:].indirect(entries(pos_sb[d], v0, UNIT)), centre[u][:], ALU.subtract
+                pull,
+                y[b][:].indirect(entries(pos_sb[d], v0 + first, width)),
+                centre[u][:, first : first + width],
+                ALU.subtract,
             )
-            for c in range(chunks):
-                turn(places[c], part(pull, c), start[c], stop[c])
 
-        def pull_into_turned(u, d, count=D, **kw):
+        def pull_and_turn(u, d, pull, count=D):
             if d == 0:
                 turned[u] = [
                     bank_tile(count * P, "turned", TURNED_BANKS[u % 2][c]) for c in range(chunks)
                 ]
-            gather_pull(
-                u, d, [part(t, d) for t in turned[u]], [d == 0] * chunks, [d == count - 1] * chunks, **kw
-            )
+            gather_pull(u, d, pull, 0, UNIT)
+            for c in range(chunks):
+                turn(part(turned[u][c], d), part(pull, c), d == 0, d == count - 1)
 
-        def clip(u, c, source, name):
+        def clip(engine, u, c, clipped, source):
             col = slice(units[u][1] // P + c, units[u][1] // P + c + 1)
-            tag = "source0_1" if (u, c) == (1, 1) else name
-            clipped = keep.tile(list(source.shape), F32, name=name, tag=tag)
-            engine = nc.gpsimd if u == 0 else nc.vector
-            engine.tensor_scalar(
-                clipped[:], source, upper[:, col], lower[:, col], ALU.min, ALU.max
-            )
-            return clipped
+            engine.tensor_scalar(clipped, source, upper[:, col], lower[:, col], ALU.min, ALU.max)
 
         def empty(u, c):
-            source = keep.tile(list(turned[u][c].shape), F32, name=f"source{u}_{c}")
-            nc.scalar.activation(source[:], turned[u][c][:], COPY, scale=1.0)
+            source = tile_after(f"source{u}_{c}", turned[u][c].shape[1])
+            nc.scalar.activation(source, turned[u][c][:], COPY, scale=1.0)
             return source
 
-        def clip_unit(u):
+        def clip_unit(engine, u, clipped):
             total[u] = bank_tile(UNIT, "total", TOTAL_BANKS[u % 2])
             for c in range(chunks):
-                clipped = clip(u, c, empty(u, c)[:], f"clipped{u}_{c}")
+                clip(engine, u, c, clipped[c], empty(u, c))
                 for d in range(D):
                     turn(
                         part(total[u], c),
-                        part(clipped, d),
+                        part(clipped[c], d),
                         c == 0 and d == 0,
                         c == chunks - 1 and d == D - 1,
                     )
@@ -225,40 +221,39 @@ def tile_picked_huber_none_e_kernel(
                 out[b * P : (b + 1) * P, v0 + first : v0 + first + width], result[:]
             )
 
+        def split(tile, width):
+            return [tile[:, i : i + width] for i in range(0, tile.shape[1], width)]
+
         gather_centre(0)
         gather_centre(1)
-        for d in range(D):
-            pull_into_turned(0, d)
-        pull_into_turned(1, 0)
-        pull_into_turned(1, 1)
-        pull_into_turned(1, 2)
+        for u in range(2):
+            for d in range(D):
+                pull_and_turn(u, d, tile_after(f"pull{u}_{d}", UNIT))
         gather_centre(2)
         gather_centre(3)
-        clip_unit(0)
-        pair = keep.tile([P, 2 * UNIT], F32, name="pair0", tag="source0_1")
-        pull_into_turned(2, 0, pull=pair[:, 0:UNIT])
-        pull_into_turned(2, 1, pull=pair[:, UNIT : 2 * UNIT])
+        clip_unit(nc.gpsimd, 0, [tile_after(f"clipped0_{c}", D * P) for c in range(chunks)])
+        for d, pull in enumerate(split(tile_after("pulls2", D * UNIT, "source0_1"), UNIT)):
+            pull_and_turn(2, d, pull)
+        clip_unit(nc.vector, 1, split(tile_after("clipped1", chunks * D * P, "clipped0_1"), D * P))
         finish(0, total[0][:], 0, UNIT)
-        clip_unit(1)
-        pair = keep.tile([P, 2 * UNIT], F32, name="pair1", tag="centre0")
-        pull_into_turned(2, 2, pull=pair[:, 0:UNIT])
-        pull_into_turned(3, 0, count=D - 1, pull=pair[:, UNIT : 2 * UNIT])
-        pull_into_turned(3, 1, count=D - 1, tag="source1_1")
+        for d, pull in enumerate(split(tile_after("pulls3", (D - 1) * UNIT, "source1_0"), UNIT)):
+            pull_and_turn(last, d, pull, count=D - 1)
+        clip_unit(nc.vector, 2, [tile_after(f"clipped2_{c}", D * P) for c in range(chunks)])
+        late = [bank_tile(P, "late", LATE_BANKS[c]) for c in range(chunks)]
+        for c, pull in enumerate(split(tile_after("late_pull", UNIT, "source2_1"), P)):
+            gather_pull(last, D - 1, pull, c * P, P)
+            turn(late[c][:], pull, True, True)
         finish(1, total[1][:], 0, UNIT)
-        clip_unit(2)
-        late = bank_tile(UNIT, "late", LATE_BANK)
-        gather_pull(
-            last, D - 1, [part(late, c) for c in range(chunks)], [True, False], [False, True],
-            tag="source2_0",
-        )
         sums = [bank_tile(P, "sums", LAST_BANKS[c]) for c in range(chunks)]
         for c in range(chunks):
-            clipped = clip(last, c, empty(last, c)[:], f"early{c}")
+            early = tile_after(f"early{c}", (D - 1) * P)
+            clip(nc.vector, last, c, early, empty(last, c))
             for d in range(D - 1):
-                turn(sums[c][:], part(clipped, d), d == 0, False)
-        finish(2, total[2][:], 0, UNIT)
+                turn(sums[c][:], part(early, d), d == 0, False)
         for c in range(chunks):
-            clipped = clip(last, c, part(late, c), f"late{c}")
-            turn(sums[c][:], clipped[:], False, True)
+            clipped = tile_after(f"late{c}", P)
+            clip(nc.vector, last, c, clipped, late[c][:])
+            turn(sums[c][:], clipped, False, True)
+        finish(2, total[2][:], 0, UNIT)
         for c in range(chunks):
             finish(last, sums[c][:], c * P, P)

@@ -31,7 +31,7 @@ LAST_PIECES = [
     (1024, "scalar"),
     (640, "vector"),
     (256, "vector"),
-    (128, "vector"),
+    (128, "scalar"),
 ]
 FIRST_BLOCK_STEPS = [
     (0, 0, 256, "scalar"),
@@ -43,8 +43,8 @@ FIRST_BLOCK_STEPS = [
 SECOND_BLOCK_BANK = len(FIRST_BLOCK_STEPS) - 2
 BOUND_BANK = 7
 TURNED_BANKS = [(0, 1), (2, 5)]
-TOTAL_BANKS = [6, 7]
-LATE_BANKS = [3, 4]
+TOTAL_BANKS = [6, 7, 4]
+LATE_BANK = 3
 LAST_BANKS = [0, 1]
 UNIT = 256
 
@@ -162,7 +162,8 @@ def tile_picked_huber_none_e_kernel(
         units = [(b, v0) for b in range(N // P) for v0 in range(0, V, UNIT)]
         chunks = UNIT // P
         last = len(units) - 1
-        centre, turned, total = {}, {}, {}
+        centre, turned = {}, {}
+        total = [bank_tile(UNIT, "total", bank)[:] for bank in TOTAL_BANKS]
 
         def tile_after(name, width, tag=None):
             return keep.tile([P, width], F32, name=name, tag=tag or name)[:]
@@ -200,7 +201,6 @@ def tile_picked_huber_none_e_kernel(
             return source
 
         def clip_unit(engine, u, clipped):
-            total[u] = bank_tile(UNIT, "total", TOTAL_BANKS[u % 2])
             for c in range(chunks):
                 clip(engine, u, c, clipped[c], empty(u, c))
                 for d in range(D):
@@ -211,14 +211,15 @@ def tile_picked_huber_none_e_kernel(
                         c == chunks - 1 and d == D - 1,
                     )
 
-        def finish(u, sums, first, width):
+        def finish(u, sums, first, width, result=None):
             b, v0 = units[u]
-            result = keep.tile([P, width], F32, name=f"result{u}_{first}")
+            if result is None:
+                result = tile_after(f"result{u}_{first}", width)
             nc.vector.scalar_tensor_tensor(
-                result[:], sums, 1.0 / D, centre[u][:, first : first + width], ALU.mult, ALU.add
+                result, sums, 1.0 / D, centre[u][:, first : first + width], ALU.mult, ALU.add
             )
             nc.sync.dma_start(
-                out[b * P : (b + 1) * P, v0 + first : v0 + first + width], result[:]
+                out[b * P : (b + 1) * P, v0 + first : v0 + first + width], result
             )
 
         def split(tile, width):
@@ -235,25 +236,25 @@ def tile_picked_huber_none_e_kernel(
         for d, pull in enumerate(split(tile_after("pulls2", D * UNIT, "source0_1"), UNIT)):
             pull_and_turn(2, d, pull)
         clip_unit(nc.vector, 1, split(tile_after("clipped1", chunks * D * P, "clipped0_1"), D * P))
-        finish(0, total[0][:], 0, UNIT)
-        for d, pull in enumerate(split(tile_after("pulls3", (D - 1) * UNIT, "source1_0"), UNIT)):
-            pull_and_turn(last, d, pull, count=D - 1)
+        for d in range(D - 1):
+            pull_and_turn(last, d, tile_after(f"pull3_{d}", UNIT, f"source1_{d}"), count=D - 1)
         clip_unit(nc.vector, 2, [tile_after(f"clipped2_{c}", D * P) for c in range(chunks)])
-        late = [bank_tile(P, "late", LATE_BANKS[c]) for c in range(chunks)]
-        for c, pull in enumerate(split(tile_after("late_pull", UNIT, "source2_1"), P)):
-            gather_pull(last, D - 1, pull, c * P, P)
-            turn(late[c][:], pull, True, True)
-        finish(1, total[1][:], 0, UNIT)
+        late = bank_tile(UNIT, "late", LATE_BANK)
+        shared = tile_after("shared", 2 * UNIT, "source1_0")
+        gather_pull(last, D - 1, shared[:, 0:UNIT], 0, UNIT)
+        for c in range(chunks):
+            turn(part(late, c), part(shared, c), c == 0, c == chunks - 1)
+        finish(0, total[0], 0, UNIT, shared[:, UNIT : 2 * UNIT])
         sums = [bank_tile(P, "sums", LAST_BANKS[c]) for c in range(chunks)]
         for c in range(chunks):
             early = tile_after(f"early{c}", (D - 1) * P)
             clip(nc.vector, last, c, early, empty(last, c))
             for d in range(D - 1):
                 turn(sums[c][:], part(early, d), d == 0, False)
-        for c in range(chunks):
             clipped = tile_after(f"late{c}", P)
-            clip(nc.vector, last, c, clipped, late[c][:])
+            clip(nc.vector, last, c, clipped, part(late, c))
             turn(sums[c][:], clipped, False, True)
-        finish(2, total[2][:], 0, UNIT)
+        finish(1, total[1], 0, UNIT, tile_after("result1", UNIT, "early0"))
+        finish(2, total[2], 0, UNIT)
         for c in range(chunks):
             finish(last, sums[c][:], c * P, P)

@@ -44,8 +44,8 @@ SECOND_BLOCK_BANK = len(FIRST_BLOCK_STEPS) - 2
 BOUND_BANK = 7
 TURNED_BANKS = [(0, 1), (2, 5)]
 TOTAL_BANKS = [6, 7, 4]
-LATE_BANK = 3
-LAST_BANKS = [0, 1]
+LAST_TOTAL_BANKS = [0, 1]
+THIRD_PULL_BANK = 3
 UNIT = 256
 
 
@@ -165,42 +165,44 @@ def tile_picked_huber_none_e_kernel(
         centre, turned = {}, {}
         total = [bank_tile(UNIT, "total", bank)[:] for bank in TOTAL_BANKS]
 
-        def tile_after(name, width, tag=None):
-            return keep.tile([P, width], F32, name=name, tag=tag or name)[:]
+        def sbuf_tile(name, width, after=None):
+            return keep.tile([P, width], F32, name=name, tag=after or name)[:]
+
+        def split(tile, width):
+            return [tile[:, i : i + width] for i in range(0, tile.shape[1], width)]
+
+        def picked_by(list_tile, u):
+            b, v0 = units[u]
+            return y[b][:].indirect(entries(list_tile, v0, UNIT))
 
         def gather_centre(u):
-            b, v0 = units[u]
-            centre[u] = tile_after(f"centre{u}", UNIT)
-            nc.vector.tensor_copy(centre[u], y[b][:].indirect(entries(cen_sb, v0, UNIT)))
+            centre[u] = sbuf_tile(f"centre{u}", UNIT)
+            nc.vector.tensor_copy(centre[u], picked_by(cen_sb, u))
 
-        def gather_pull(u, d, pull, first, width):
-            b, v0 = units[u]
-            nc.vector.tensor_tensor(
-                pull,
-                y[b][:].indirect(entries(pos_sb[d], v0 + first, width)),
-                centre[u][:, first : first + width],
-                ALU.subtract,
-            )
+        def gather_pull(u, d, pull):
+            nc.vector.tensor_tensor(pull, picked_by(pos_sb[d], u), centre[u], ALU.subtract)
+
+        def turned_banks(u, count):
+            return [bank_tile(count * P, "turned", TURNED_BANKS[u % 2][c]) for c in range(chunks)]
 
         def pull_and_turn(u, d, pull, count=D):
             if d == 0:
-                turned[u] = [
-                    bank_tile(count * P, "turned", TURNED_BANKS[u % 2][c]) for c in range(chunks)
-                ]
-            gather_pull(u, d, pull, 0, UNIT)
+                turned[u] = turned_banks(u, count)
+            gather_pull(u, d, pull)
             for c in range(chunks):
                 turn(part(turned[u][c], d), part(pull, c), d == 0, d == count - 1)
+
+        def empty(u, c):
+            source = sbuf_tile(f"source{u}_{c}", turned[u][c].shape[1])
+            nc.scalar.activation(source, turned[u][c][:], COPY, scale=1.0)
+            return source
 
         def clip(engine, u, c, clipped, source):
             col = slice(units[u][1] // P + c, units[u][1] // P + c + 1)
             engine.tensor_scalar(clipped, source, upper[:, col], lower[:, col], ALU.min, ALU.max)
 
-        def empty(u, c):
-            source = tile_after(f"source{u}_{c}", turned[u][c].shape[1])
-            nc.scalar.activation(source, turned[u][c][:], COPY, scale=1.0)
-            return source
-
-        def clip_unit(engine, u, clipped):
+        def clip_unit(engine, u):
+            clipped = [sbuf_tile(f"clipped{u}_{c}", D * P) for c in range(chunks)]
             for c in range(chunks):
                 clip(engine, u, c, clipped[c], empty(u, c))
                 for d in range(D):
@@ -211,50 +213,58 @@ def tile_picked_huber_none_e_kernel(
                         c == chunks - 1 and d == D - 1,
                     )
 
-        def finish(u, sums, first, width, result=None):
+        def finish(u, sums, first, result):
             b, v0 = units[u]
-            if result is None:
-                result = tile_after(f"result{u}_{first}", width)
+            cols = slice(first, first + result.shape[1])
             nc.vector.scalar_tensor_tensor(
-                result, sums, 1.0 / D, centre[u][:, first : first + width], ALU.mult, ALU.add
+                result, sums, 1.0 / D, centre[u][:, cols], ALU.mult, ALU.add
             )
-            nc.sync.dma_start(
-                out[b * P : (b + 1) * P, v0 + first : v0 + first + width], result
-            )
-
-        def split(tile, width):
-            return [tile[:, i : i + width] for i in range(0, tile.shape[1], width)]
+            nc.sync.dma_start(out[b * P : (b + 1) * P, v0 + cols.start : v0 + cols.stop], result)
 
         gather_centre(0)
         gather_centre(1)
         for u in range(2):
             for d in range(D):
-                pull_and_turn(u, d, tile_after(f"pull{u}_{d}", UNIT))
+                pull_and_turn(u, d, sbuf_tile(f"pull{u}_{d}", UNIT))
+
         gather_centre(2)
         gather_centre(3)
-        clip_unit(nc.gpsimd, 0, [tile_after(f"clipped0_{c}", D * P) for c in range(chunks)])
-        for d, pull in enumerate(split(tile_after("pulls2", D * UNIT, "source0_1"), UNIT)):
-            pull_and_turn(2, d, pull)
-        clip_unit(nc.vector, 1, split(tile_after("clipped1", chunks * D * P, "clipped0_1"), D * P))
+        clip_unit(nc.gpsimd, 0)
+
+        negated = sbuf_tile("negated", UNIT)
+        nc.scalar.activation(negated, centre[2], COPY, scale=-1.0)
+        turned[2] = turned_banks(2, D)
+        for c in range(chunks):
+            for d in range(1, D):
+                turn(part(turned[2][c], d), part(negated, c), d == 1, False)
+        for d, gathered in enumerate(split(sbuf_tile("pulls2", D * UNIT, after="source0_0"), UNIT)):
+            if d == 0:
+                gather_pull(2, d, gathered)
+            else:
+                nc.vector.tensor_copy(gathered, picked_by(pos_sb[d], 2))
+            for c in range(chunks):
+                turn(part(turned[2][c], d), part(gathered, c), False, d == D - 1)
+        clip_unit(nc.gpsimd, 1)
+
+        pulls = split(sbuf_tile("last_pulls", D * UNIT, after="source1_0"), UNIT)
         for d in range(D - 1):
-            pull_and_turn(last, d, tile_after(f"pull3_{d}", UNIT, f"source1_{d}"), count=D - 1)
-        clip_unit(nc.vector, 2, [tile_after(f"clipped2_{c}", D * P) for c in range(chunks)])
-        late = bank_tile(UNIT, "late", LATE_BANK)
-        shared = tile_after("shared", 2 * UNIT, "source1_0")
-        gather_pull(last, D - 1, shared[:, 0:UNIT], 0, UNIT)
+            pull_and_turn(last, d, pulls[d], count=D - 1)
+        third = bank_tile(UNIT, "third", THIRD_PULL_BANK)
+        gather_pull(last, D - 1, pulls[D - 1])
         for c in range(chunks):
-            turn(part(late, c), part(shared, c), c == 0, c == chunks - 1)
-        finish(0, total[0], 0, UNIT, shared[:, UNIT : 2 * UNIT])
-        sums = [bank_tile(P, "sums", LAST_BANKS[c]) for c in range(chunks)]
+            turn(part(third, c), part(pulls[D - 1], c), c == 0, c == chunks - 1)
+        clip_unit(nc.vector, 2)
+        finish(0, total[0], 0, sbuf_tile("result0", UNIT, after="source2_0"))
+        last_total = [bank_tile(P, "last_total", LAST_TOTAL_BANKS[c]) for c in range(chunks)]
         for c in range(chunks):
-            early = tile_after(f"early{c}", (D - 1) * P)
-            clip(nc.vector, last, c, early, empty(last, c))
+            first_two = sbuf_tile(f"first_two{c}", (D - 1) * P)
+            clip(nc.vector, last, c, first_two, empty(last, c))
             for d in range(D - 1):
-                turn(sums[c][:], part(early, d), d == 0, False)
-            clipped = tile_after(f"late{c}", P)
-            clip(nc.vector, last, c, clipped, part(late, c))
-            turn(sums[c][:], clipped, False, True)
-        finish(1, total[1], 0, UNIT, tile_after("result1", UNIT, "early0"))
-        finish(2, total[2], 0, UNIT)
+                turn(last_total[c][:], part(first_two, d), d == 0, False)
+            third_clipped = sbuf_tile(f"third_clipped{c}", P)
+            clip(nc.vector, last, c, third_clipped, part(third, c))
+            turn(last_total[c][:], third_clipped, False, True)
+        finish(1, total[1], 0, sbuf_tile("result1", UNIT, after="first_two0"))
+        finish(2, total[2], 0, sbuf_tile("result2", UNIT))
         for c in range(chunks):
-            finish(last, sums[c][:], c * P, P)
+            finish(last, last_total[c][:], c * P, sbuf_tile(f"result{last}_{c}", P))

@@ -43,7 +43,9 @@ FIRST_BLOCK_STEPS = [
 SECOND_BLOCK_BANK = len(FIRST_BLOCK_STEPS) - 2
 BOUND_BANK = 7
 TURNED_BANKS = [(0, 1), (2, 5)]
-TOTAL_BANKS = [6, 7, 4]
+FIRST_TOTAL_BANK = 6
+CENTRE_BANK = 7
+THIRD_UNIT_TOTAL_BANK = 4
 LAST_TOTAL_BANKS = [0, 1]
 THIRD_PULL_BANK = 3
 UNIT = 256
@@ -163,7 +165,9 @@ def tile_picked_huber_none_e_kernel(
         chunks = UNIT // P
         last = len(units) - 1
         centre, turned = {}, {}
-        total = [bank_tile(UNIT, "total", bank)[:] for bank in TOTAL_BANKS]
+        first_total = bank_tile(V, "first_total", FIRST_TOTAL_BANK)[:]
+        total = [first_total[:, :UNIT], first_total[:, UNIT:]]
+        total.append(bank_tile(UNIT, "total", THIRD_UNIT_TOTAL_BANK)[:])
 
         def sbuf_tile(name, width, after=None):
             return keep.tile([P, width], F32, name=name, tag=after or name)[:]
@@ -209,8 +213,8 @@ def tile_picked_huber_none_e_kernel(
                     turn(
                         part(total[u], c),
                         part(clipped[c], d),
-                        c == 0 and d == 0,
-                        c == chunks - 1 and d == D - 1,
+                        u == 2 and c == 0 and d == 0,
+                        u >= 1 and c == chunks - 1 and d == D - 1,
                     )
 
         def finish(u, sums, first, result):
@@ -223,6 +227,13 @@ def tile_picked_huber_none_e_kernel(
 
         gather_centre(0)
         gather_centre(1)
+        centre_t = bank_tile(V, "centre_t", CENTRE_BANK)
+        for c in range(V // P):
+            turn(part(centre_t, c), part(centre[c // chunks], c % chunks), c == 0, c == V // P - 1)
+        tripled = sbuf_tile("tripled", V)
+        nc.scalar.activation(tripled, centre_t[:], COPY, scale=float(D))
+        for c in range(V // P):
+            turn(part(first_total, c), part(tripled, c), c == 0, False)
         for u in range(2):
             for d in range(D):
                 pull_and_turn(u, d, sbuf_tile(f"pull{u}_{d}", UNIT))
@@ -233,28 +244,43 @@ def tile_picked_huber_none_e_kernel(
 
         negated = sbuf_tile("negated", UNIT)
         nc.scalar.activation(negated, centre[2], COPY, scale=-1.0)
-        turned[2] = turned_banks(2, D)
+        turned[2] = turned_banks(2, D - 1)
+        third2 = bank_tile(UNIT, "third2", CENTRE_BANK)
         for c in range(chunks):
-            for d in range(1, D):
-                turn(part(turned[2][c], d), part(negated, c), d == 1, False)
+            turn(part(turned[2][c], 1), part(negated, c), True, False)
+        for c in range(chunks):
+            turn(part(third2, c), part(negated, c), c == 0, False)
         for d, gathered in enumerate(split(sbuf_tile("pulls2", D * UNIT, after="source0_0"), UNIT)):
             if d == 0:
                 gather_pull(2, d, gathered)
             else:
                 nc.vector.tensor_copy(gathered, picked_by(pos_sb[d], 2))
             for c in range(chunks):
-                turn(part(turned[2][c], d), part(gathered, c), False, d == D - 1)
+                if d < D - 1:
+                    turn(part(turned[2][c], d), part(gathered, c), False, d == D - 2)
+                else:
+                    turn(part(third2, c), part(gathered, c), False, c == chunks - 1)
         clip_unit(nc.gpsimd, 1)
 
-        pulls = split(sbuf_tile("last_pulls", D * UNIT, after="source1_0"), UNIT)
+        pulls = split(sbuf_tile("last_pulls", (D - 1) * UNIT, after="source1_0"), UNIT)
         for d in range(D - 1):
             pull_and_turn(last, d, pulls[d], count=D - 1)
+        for c in range(chunks):
+            early = sbuf_tile(f"early2_{c}", (D - 1) * P)
+            clip(nc.vector, 2, c, early, empty(2, c))
+            for d in range(D - 1):
+                turn(part(total[2], c), part(early, d), c == 0 and d == 0, False)
+        third2_source = sbuf_tile("third2_source", UNIT)
+        nc.scalar.activation(third2_source, third2[:], COPY, scale=1.0)
+        pulls.append(sbuf_tile("last_pull", UNIT, after="source2_0"))
         third = bank_tile(UNIT, "third", THIRD_PULL_BANK)
         gather_pull(last, D - 1, pulls[D - 1])
         for c in range(chunks):
             turn(part(third, c), part(pulls[D - 1], c), c == 0, c == chunks - 1)
-        clip_unit(nc.vector, 2)
-        finish(0, total[0], 0, sbuf_tile("result0", UNIT, after="source2_0"))
+        for c in range(chunks):
+            late = sbuf_tile(f"late2_{c}", P)
+            clip(nc.vector, 2, c, late, part(third2_source, c))
+            turn(part(total[2], c), late, False, c == chunks - 1)
         last_total = [bank_tile(P, "last_total", LAST_TOTAL_BANKS[c]) for c in range(chunks)]
         for c in range(chunks):
             first_two = sbuf_tile(f"first_two{c}", (D - 1) * P)
@@ -264,7 +290,9 @@ def tile_picked_huber_none_e_kernel(
             third_clipped = sbuf_tile(f"third_clipped{c}", P)
             clip(nc.vector, last, c, third_clipped, part(third, c))
             turn(last_total[c][:], third_clipped, False, True)
-        finish(1, total[1], 0, sbuf_tile("result1", UNIT, after="first_two0"))
+        first_result = sbuf_tile("first_result", V)
+        nc.scalar.activation(first_result, first_total, COPY, scale=1.0 / D)
+        nc.sync.dma_start(out[0:P, :], first_result)
         finish(2, total[2], 0, sbuf_tile("result2", UNIT))
         for c in range(chunks):
             finish(last, last_total[c][:], c * P, sbuf_tile(f"result{last}_{c}", P))

@@ -41,7 +41,6 @@ FIRST_BLOCK_STEPS = [
     (1, 384, 128, "vector"),
 ]
 SECOND_BLOCK_BANK = len(FIRST_BLOCK_STEPS) - 2
-BOUND_BANK = 7
 TURNED_BANKS = [(0, 1), (2, 5)]
 FIRST_TOTAL_BANK = 6
 CENTRE_BANK = 7
@@ -81,8 +80,6 @@ def tile_picked_huber_none_e_kernel(
 
         w_scales = keep.tile([P, N], U8, name="w_scales", align_bytes=64)
         nc.vector.memset(w_scales[:].bitcast(I32), 0)
-        bound_rows = keep.tile([P, P], F32, name="bound_rows")
-        nc.vector.memset(bound_rows[:], 0.0)
         ident = keep.tile([P, P], F32, name="ident")
         make_identity(nc, ident[:])
 
@@ -90,7 +87,6 @@ def tile_picked_huber_none_e_kernel(
         planes = [keep.tile([P, T], F32, name=f"plane{t}") for t in range(PACK)]
         nc.sync.dma_start(planes[0][:], rows[:, 0, :])
         offs_sb = load_list(offs, "offs_sb")
-        nc.sync.dma_start(bound_rows[0 : V // P, :], bound[0].rearrange("(c p) -> c p", p=P))
         for t in range(1, LAST):
             nc.sync.dma_start(planes[t][:], rows[:, t, :])
         pieces = []
@@ -103,19 +99,18 @@ def tile_picked_huber_none_e_kernel(
         w_words = keep.tile([P, 2 * N], U8, name="w_words", align_bytes=64)
         nc.sync.dma_start(w_words[:], w1_words[0])
         for q in range(P // QUADRANT):
-            nc.gpsimd.dma_start(
+            nc.sync.dma_start(
                 w_scales[QUADRANT * q : QUADRANT * q + 4, :].bitcast(I32),
                 w1_scales[0, 4 * q : 4 * q + 4, :].bitcast(I32),
             )
-        cen_sb = load_list(cen, "cen_sb")
         pos_sb = [load_list(src, f"pos{d}_sb") for d, src in enumerate((pos1, pos2, pos3))]
+        cen_sb = load_list(cen, "cen_sb")
 
-        bound_t = bank_tile(P, "bound_t", BOUND_BANK)
-        nc.tensor.transpose(bound_t[:], bound_rows[:], ident[:])
         upper = keep.tile([P, V // P], F32, name="upper")
         lower = keep.tile([P, V // P], F32, name="lower")
-        nc.scalar.activation(upper[:], bound_t[:, 0 : V // P], COPY, scale=1.0)
-        nc.scalar.activation(lower[:], bound_t[:, 0 : V // P], COPY, scale=-1.0)
+        with nc.allow_non_contiguous_dma(reason="512 bounds, one target a partition"):
+            nc.sync.dma_start(upper[:], bound[0].rearrange("(c p) -> p c", p=P))
+        nc.gpsimd.tensor_scalar(lower[:], upper[:], -1.0, 0.0, ALU.mult, ALU.add)
 
         picked = [
             keep.tile([P, HALF, PACK], BF16, name=f"picked{h}", align_bytes=64) for h in range(2)

@@ -41,12 +41,6 @@ FIRST_BLOCK_STEPS = [
     (1, 384, 128, "vector"),
 ]
 SECOND_BLOCK_BANK = len(FIRST_BLOCK_STEPS) - 2
-TURNED_BANKS = [(0, 1), (2, 5)]
-FIRST_TOTAL_BANK = 6
-CENTRE_BANK = 7
-THIRD_UNIT_TOTAL_BANK = 4
-LAST_TOTAL_BANKS = [0, 1]
-THIRD_PULL_BANK = 3
 UNIT = 256
 
 
@@ -96,6 +90,8 @@ def tile_picked_huber_none_e_kernel(
             nc.sync.dma_start(planes[LAST][:, cols], rows[:, LAST, cols])
             pieces.append((cols, engine))
             first += width
+        cen_sb = load_list(cen, "cen_sb")
+        pos_sb = [load_list(pos1, "pos0_sb")]
         w_words = keep.tile([P, 2 * N], U8, name="w_words", align_bytes=64)
         nc.sync.dma_start(w_words[:], w1_words[0])
         for q in range(P // QUADRANT):
@@ -103,14 +99,14 @@ def tile_picked_huber_none_e_kernel(
                 w_scales[QUADRANT * q : QUADRANT * q + 4, :].bitcast(I32),
                 w1_scales[0, 4 * q : 4 * q + 4, :].bitcast(I32),
             )
-        pos_sb = [load_list(src, f"pos{d}_sb") for d, src in enumerate((pos1, pos2, pos3))]
-        cen_sb = load_list(cen, "cen_sb")
+        pos_sb.append(load_list(pos2, "pos1_sb"))
+        pos_sb.append(load_list(pos3, "pos2_sb"))
 
         upper = keep.tile([P, V // P], F32, name="upper")
         lower = keep.tile([P, V // P], F32, name="lower")
         with nc.allow_non_contiguous_dma(reason="512 bounds, one target a partition"):
             nc.sync.dma_start(upper[:], bound[0].rearrange("(c p) -> p c", p=P))
-        nc.gpsimd.tensor_scalar(lower[:], upper[:], -1.0, 0.0, ALU.mult, ALU.add)
+        nc.scalar.activation(lower[:], upper[:], COPY, scale=-1.0)
 
         picked = [
             keep.tile([P, HALF, PACK], BF16, name=f"picked{h}", align_bytes=64) for h in range(2)
@@ -129,7 +125,7 @@ def tile_picked_huber_none_e_kernel(
         scales = [keep.tile([P, HALF], U8, name=f"scales{h}", align_bytes=64) for h in range(2)]
         y = [keep.tile([P, S], F32, name=f"y{b}") for b in range(N // P)]
 
-        def project(b, h, cols, bank, engine):
+        def product(b, h, cols, bank):
             acc = bank_tile(cols.stop - cols.start, "acc", bank)
             nc.tensor.matmul_mx(
                 out=acc[:],
@@ -140,6 +136,9 @@ def tile_picked_huber_none_e_kernel(
                 start=True,
                 stop=True,
             )
+            return acc
+
+        def bring_out(b, h, cols, acc, engine):
             copy_on(engine, y[b][:, h * HALF + cols.start : h * HALF + cols.stop], acc[:])
 
         for bank, (h, first, width, engine) in enumerate(FIRST_BLOCK_STEPS):
@@ -149,145 +148,148 @@ def tile_picked_huber_none_e_kernel(
                 scales=scales[h][:, cols],
                 in_=picked[h][:, cols, :].rearrange("p j t -> p (j t)"),
             )
-            project(0, h, cols, bank, engine)
-        for h in range(2):
-            project(1, h, slice(0, HALF), SECOND_BLOCK_BANK + h, "scalar")
+            bring_out(0, h, cols, product(0, h, cols, bank), engine)
+        whole = slice(0, HALF)
+        second = [product(1, h, whole, SECOND_BLOCK_BANK + h) for h in range(2)]
 
         def turn(dst, src, start, stop):
             nc.tensor.matmul(dst, src, ident[:], start=start, stop=stop, is_transpose=True)
 
         units = [(b, v0) for b in range(N // P) for v0 in range(0, V, UNIT)]
         chunks = UNIT // P
-        last = len(units) - 1
-        centre, turned = {}, {}
-        first_total = bank_tile(V, "first_total", FIRST_TOTAL_BANK)[:]
-        total = [first_total[:, :UNIT], first_total[:, UNIT:]]
-        total.append(bank_tile(UNIT, "total", THIRD_UNIT_TOTAL_BANK)[:])
 
         def sbuf_tile(name, width, after=None):
             return keep.tile([P, width], F32, name=name, tag=after or name)[:]
-
-        def split(tile, width):
-            return [tile[:, i : i + width] for i in range(0, tile.shape[1], width)]
 
         def picked_by(list_tile, u):
             b, v0 = units[u]
             return y[b][:].indirect(entries(list_tile, v0, UNIT))
 
-        def gather_centre(u):
-            centre[u] = sbuf_tile(f"centre{u}", UNIT)
-            nc.vector.tensor_copy(centre[u], picked_by(cen_sb, u))
+        negated = {}
 
-        def gather_pull(u, d, pull):
-            nc.vector.tensor_tensor(pull, picked_by(pos_sb[d], u), centre[u], ALU.subtract)
+        def minus_centre(u):
+            return negated[u]
 
-        def turned_banks(u, count):
-            return [bank_tile(count * P, "turned", TURNED_BANKS[u % 2][c]) for c in range(chunks)]
+        def gather_centre(u, dst=None):
+            negated[u] = sbuf_tile(f"negated{u}", UNIT) if dst is None else dst
+            nc.scalar.activation(minus_centre(u), picked_by(cen_sb, u), COPY, scale=-1.0)
 
-        def pull_and_turn(u, d, pull, count=D):
-            if d == 0:
-                turned[u] = turned_banks(u, count)
-            gather_pull(u, d, pull)
-            for c in range(chunks):
-                turn(part(turned[u][c], d), part(pull, c), d == 0, d == count - 1)
+        def group(name, width, bank, count):
+            return {"tile": bank_tile(width, name, bank)[:], "left": count, "count": count}
 
-        def empty(u, c):
-            source = sbuf_tile(f"source{u}_{c}", turned[u][c].shape[1])
-            nc.scalar.activation(source, turned[u][c][:], COPY, scale=1.0)
-            return source
+        def turn_into(g, i, src):
+            g["left"] -= 1
+            turn(part(g["tile"], i), src, g["left"] == g["count"] - 1, g["left"] == 0)
 
-        def clip(engine, u, c, clipped, source):
-            col = slice(units[u][1] // P + c, units[u][1] // P + c + 1)
-            engine.tensor_scalar(clipped, source, upper[:, col], lower[:, col], ALU.min, ALU.max)
-
-        def clip_unit(engine, u):
-            clipped = [sbuf_tile(f"clipped{u}_{c}", D * P) for c in range(chunks)]
-            for c in range(chunks):
-                clip(engine, u, c, clipped[c], empty(u, c))
-                for d in range(D):
-                    turn(
-                        part(total[u], c),
-                        part(clipped[c], d),
-                        u == 2 and c == 0 and d == 0,
-                        u >= 1 and c == chunks - 1 and d == D - 1,
-                    )
-
-        def finish(u, sums, first, result):
-            b, v0 = units[u]
-            cols = slice(first, first + result.shape[1])
-            nc.vector.scalar_tensor_tensor(
-                result, sums, 1.0 / D, centre[u][:, cols], ALU.mult, ALU.add
-            )
-            nc.sync.dma_start(out[b * P : (b + 1) * P, v0 + cols.start : v0 + cols.stop], result)
-
-        gather_centre(0)
-        gather_centre(1)
-        centre_t = bank_tile(V, "centre_t", CENTRE_BANK)
-        for c in range(V // P):
-            turn(part(centre_t, c), part(centre[c // chunks], c % chunks), c == 0, c == V // P - 1)
-        tripled = sbuf_tile("tripled", V)
-        nc.scalar.activation(tripled, centre_t[:], COPY, scale=float(D))
-        for c in range(V // P):
-            turn(part(first_total, c), part(tripled, c), c == 0, False)
-        for u in range(2):
-            for d in range(D):
-                pull_and_turn(u, d, sbuf_tile(f"pull{u}_{d}", UNIT))
-
-        gather_centre(2)
-        gather_centre(3)
-        clip_unit(nc.gpsimd, 0)
-
-        negated = sbuf_tile("negated", UNIT)
-        nc.scalar.activation(negated, centre[2], COPY, scale=-1.0)
-        turned[2] = turned_banks(2, D - 1)
-        third2 = bank_tile(UNIT, "third2", CENTRE_BANK)
-        for c in range(chunks):
-            turn(part(turned[2][c], 1), part(negated, c), True, False)
-        for c in range(chunks):
-            turn(part(third2, c), part(negated, c), c == 0, False)
-        for d, gathered in enumerate(split(sbuf_tile("pulls2", D * UNIT, after="source0_0"), UNIT)):
-            if d == 0:
-                gather_pull(2, d, gathered)
+        def gather_plain(engine, u, d, after=None, dst=None):
+            if dst is None:
+                dst = sbuf_tile(f"gathered{u}_{d}", UNIT, after)
+            if engine == "vector":
+                nc.vector.tensor_copy(dst, picked_by(pos_sb[d], u))
             else:
-                nc.vector.tensor_copy(gathered, picked_by(pos_sb[d], 2))
-            for c in range(chunks):
-                if d < D - 1:
-                    turn(part(turned[2][c], d), part(gathered, c), False, d == D - 2)
-                else:
-                    turn(part(third2, c), part(gathered, c), False, c == chunks - 1)
-        clip_unit(nc.gpsimd, 1)
+                nc.scalar.activation(dst, picked_by(pos_sb[d], u), COPY)
+            return dst
 
-        pulls = split(sbuf_tile("last_pulls", (D - 1) * UNIT, after="source1_0"), UNIT)
-        for d in range(D - 1):
-            pull_and_turn(last, d, pulls[d], count=D - 1)
+        def gather_pull(u, d, after=None, dst=None):
+            if dst is None:
+                dst = sbuf_tile(f"gathered{u}_{d}", UNIT, after)
+            nc.vector.tensor_tensor(dst, picked_by(pos_sb[d], u), minus_centre(u), ALU.add)
+            return dst
+
+        def turn_chunks(groups, i, src):
+            for c in range(chunks):
+                turn_into(groups[c], i, part(src, c))
+
+        def clip(u, c, source, name, engine=nc.vector):
+            col = slice(units[u][1] // P + c, units[u][1] // P + c + 1)
+            clipped = sbuf_tile(name, source.shape[1])
+            engine.tensor_scalar(clipped, source, upper[:, col], lower[:, col], ALU.min, ALU.max)
+            return clipped
+
+        def clip_back(u, c, source, name, total, i, engine=nc.vector):
+            clipped = clip(u, c, source, name, engine)
+            for d in range(source.shape[1] // P):
+                turn_into(total, i, part(clipped, d))
+            return clipped
+
+        def empty(source, name):
+            dst = sbuf_tile(name, source.shape[1])
+            nc.scalar.copy(dst, source)
+            return dst
+
+        def mean(u, first, sums, result):
+            cols = slice(first, first + sums.shape[1])
+            nc.vector.scalar_tensor_tensor(
+                result, sums, 1.0 / D, negated[u][:, cols], ALU.mult, ALU.subtract
+            )
+
+        def finish(u, first, sums):
+            b, v0 = units[u]
+            width = sums.shape[1]
+            result = sbuf_tile(f"result{u}_{first}", width)
+            mean(u, first, sums, result)
+            nc.sync.dma_start(out[b * P : (b + 1) * P, v0 + first : v0 + first + width], result)
+
+        def pair(name, after):
+            tile = sbuf_tile(name, 2 * UNIT, after)
+            return tile[:, :UNIT], tile[:, UNIT:]
+
+        def turned(u, banks, pulls, plain):
+            return [group(f"turned{u}_{c}", pulls * P, banks[c], pulls + plain) for c in range(chunks)]
+
+        t0 = turned(0, (0, 1), 3, 1)
+        t1 = turned(1, (2, 5), 3, 1)
+        total0 = group("total0", V, 6, 12)
+        gather_centre(0)
+        turn_chunks(t0, 0, gather_plain("vector", 0, 0))
+        turn_chunks(t0, 0, minus_centre(0))
+        turn_chunks(t0, 1, gather_pull(0, 1))
+        gather_centre(1)
+        turn_chunks(t1, 0, minus_centre(1))
+        turn_chunks(t1, 0, gather_plain("scalar", 1, 0))
+        turn_chunks(t0, 2, gather_pull(0, 2))
+        turn_chunks(t1, 1, gather_pull(1, 1))
+        for h in range(2):
+            bring_out(1, h, whole, second[h], "scalar")
+        turn_chunks(t1, 2, gather_pull(1, 2))
+        gather_centre(2)
         for c in range(chunks):
-            early = sbuf_tile(f"early2_{c}", (D - 1) * P)
-            clip(nc.vector, 2, c, early, empty(2, c))
-            for d in range(D - 1):
-                turn(part(total[2], c), part(early, d), c == 0 and d == 0, False)
-        third2_source = sbuf_tile("third2_source", UNIT)
-        nc.scalar.activation(third2_source, third2[:], COPY, scale=1.0)
-        pulls.append(sbuf_tile("last_pull", UNIT, after="source2_0"))
-        third = bank_tile(UNIT, "third", THIRD_PULL_BANK)
-        gather_pull(last, D - 1, pulls[D - 1])
-        for c in range(chunks):
-            turn(part(third, c), part(pulls[D - 1], c), c == 0, c == chunks - 1)
-        for c in range(chunks):
-            late = sbuf_tile(f"late2_{c}", P)
-            clip(nc.vector, 2, c, late, part(third2_source, c))
-            turn(part(total[2], c), late, False, c == chunks - 1)
-        last_total = [bank_tile(P, "last_total", LAST_TOTAL_BANKS[c]) for c in range(chunks)]
-        for c in range(chunks):
-            first_two = sbuf_tile(f"first_two{c}", (D - 1) * P)
-            clip(nc.vector, last, c, first_two, empty(last, c))
-            for d in range(D - 1):
-                turn(last_total[c][:], part(first_two, d), d == 0, False)
-            third_clipped = sbuf_tile(f"third_clipped{c}", P)
-            clip(nc.vector, last, c, third_clipped, part(third, c))
-            turn(last_total[c][:], third_clipped, False, True)
+            clip_back(0, c, t0[c]["tile"], f"clipped0_{c}", total0, c)
+        t2 = turned(2, (0, 1), 3, 2)
+        for d in range(2):
+            turn_chunks(t2, d, minus_centre(2))
+        turn_chunks(t2, 0, gather_plain("scalar", 2, 0))
+        second_pull, third_pull = pair("pulls2", "clipped0_0")
+        gather_plain("scalar", 2, 1, dst=second_pull)
+        clip_back(1, 0, t1[0]["tile"], "clipped1_0", total0, 2)
+        turn_chunks(t2, 1, second_pull)
+        gather_centre(3, sbuf_tile("negated3", UNIT, "clipped0_1"))
+        got1 = clip_back(1, 1, t1[1]["tile"], "clipped1_1", total0, 3)
+        turn_chunks(t2, 2, gather_pull(2, 2, dst=third_pull))
+        t3 = turned(3, (2, 5), 2, 2)
+        for d in range(2):
+            turn_chunks(t3, d, minus_centre(3))
+        turn_chunks(t3, 0, gather_plain("scalar", 3, 0, after="clipped1_1"))
         first_result = sbuf_tile("first_result", V)
-        nc.scalar.activation(first_result, first_total, COPY, scale=1.0 / D)
+        for u in range(2):
+            cols = slice(u * UNIT, (u + 1) * UNIT)
+            mean(u, 0, total0["tile"][:, cols], first_result[:, cols])
         nc.sync.dma_start(out[0:P, :], first_result)
-        finish(2, total[2], 0, sbuf_tile("result2", UNIT))
+        total2 = group("total2", UNIT, 7, 6)
+        last_second, last_third = pair("pulls3", "clipped0_0")
+        gather_plain("scalar", 3, 1, dst=last_second)
+        t3b = [group(f"third{c}", P, (3, 4)[c], 2) for c in range(chunks)]
+        turn_chunks(t3b, 0, minus_centre(3))
+        clip_back(2, 0, t2[0]["tile"], "clipped2_0", total2, 0)
+        turn_chunks(t3, 1, last_second)
+        got = clip_back(2, 1, t2[1]["tile"], "clipped2_1", total2, 1)
+        gather_plain("scalar", 3, 2, dst=last_third)
+        total3 = [group(f"total3_{c}", P, (0, 1)[c], 3) for c in range(chunks)]
+        clip_back(3, 0, t3[0]["tile"], "clipped3_0", total3[0], 0)
+        turn_chunks(t3b, 0, last_third)
+        clip_back(3, 1, t3[1]["tile"], "clipped3_1", total3[1], 0)
+        finish(2, 0, total2["tile"])
         for c in range(chunks):
-            finish(last, last_total[c][:], c * P, sbuf_tile(f"result{last}_{c}", P))
+            clip_back(3, c, t3b[c]["tile"], f"clipped3b_{c}", total3[c], 0)
+        for c in range(chunks):
+            finish(3, c * P, total3[c]["tile"])

@@ -99,6 +99,8 @@ def tile_picked_huber_none_e_kernel(
                 w_scales[QUADRANT * q : QUADRANT * q + 4, :].bitcast(I32),
                 w1_scales[0, 4 * q : 4 * q + 4, :].bitcast(I32),
             )
+        far = keep.tile([P, UNIT], F32, name="far")
+        nc.sync.dma_start(far[:], bound[:, V - UNIT :])
         pos_sb.append(load_list(pos2, "pos1_sb"))
         pos_sb.append(load_list(pos3, "pos2_sb"))
 
@@ -237,59 +239,79 @@ def tile_picked_huber_none_e_kernel(
         def turned(u, banks, pulls, plain):
             return [group(f"turned{u}_{c}", pulls * P, banks[c], pulls + plain) for c in range(chunks)]
 
+        def turn_shared(g, pulls, d, src):
+            for c in range(chunks):
+                turn_into(g, pulls * c + d, part(src, c))
+
         t0 = turned(0, (0, 1), 3, 1)
-        t1 = turned(1, (2, 5), 3, 1)
-        total0 = group("total0", V, 6, 12)
+        t1 = turned(1, (2, 5), 3, 2)
+        total0 = group("total0", UNIT, 6, 6)
+        total1 = group("total1", UNIT, 7, 6)
+        last = len(units) - 1
+        reach = keep.tile([P, UNIT], F32, name="reach", tag="picked1", align_bytes=64)
+        nc.gpsimd.tensor_scalar(reach[:], far[:], 1.0 / D, 0.0, ALU.mult, ALU.add)
+
+        def gather_third(list_tile, name):
+            dst = sbuf_tile(name, UNIT)
+            nc.scalar.activation(dst, picked_by(list_tile, last), COPY, scale=1.0 / D)
+            return dst
+
         gather_centre(0)
         turn_chunks(t0, 0, gather_plain("vector", 0, 0))
         turn_chunks(t0, 0, minus_centre(0))
         turn_chunks(t0, 1, gather_pull(0, 1))
         gather_centre(1)
-        turn_chunks(t1, 0, minus_centre(1))
-        turn_chunks(t1, 0, gather_plain("scalar", 1, 0))
         turn_chunks(t0, 2, gather_pull(0, 2))
-        turn_chunks(t1, 1, gather_pull(1, 1))
+        for d in range(2):
+            turn_chunks(t1, d, minus_centre(1))
         for h in range(2):
             bring_out(1, h, whole, second[h], "scalar")
         turn_chunks(t1, 2, gather_pull(1, 2))
-        gather_centre(2)
+        for d in range(2):
+            turn_chunks(t1, d, gather_plain("scalar", 1, d))
         for c in range(chunks):
             clip_back(0, c, t0[c]["tile"], f"clipped0_{c}", total0, c)
-        t2 = turned(2, (0, 1), 3, 2)
-        for d in range(2):
-            turn_chunks(t2, d, minus_centre(2))
-        turn_chunks(t2, 0, gather_plain("scalar", 2, 0))
-        second_pull, third_pull = pair("pulls2", "clipped0_0")
-        gather_plain("scalar", 2, 1, dst=second_pull)
-        clip_back(1, 0, t1[0]["tile"], "clipped1_0", total0, 2)
-        turn_chunks(t2, 1, second_pull)
-        gather_centre(3, sbuf_tile("negated3", UNIT, "clipped0_1"))
-        got1 = clip_back(1, 1, t1[1]["tile"], "clipped1_1", total0, 3)
-        turn_chunks(t2, 2, gather_pull(2, 2, dst=third_pull))
-        t3 = turned(3, (2, 5), 2, 2)
-        for d in range(2):
-            turn_chunks(t3, d, minus_centre(3))
-        turn_chunks(t3, 0, gather_plain("scalar", 3, 0, after="clipped1_1"))
+        centre = gather_third(cen_sb, "centre")
+        high = sbuf_tile("high", UNIT)
+        low = sbuf_tile("low", UNIT)
+        nc.gpsimd.tensor_tensor(high, centre, reach[:], ALU.add)
+        nc.gpsimd.tensor_tensor(low, centre, reach[:], ALU.subtract)
+        for c in range(chunks):
+            got1 = clip_back(1, c, t1[c]["tile"], f"clipped1_{c}", total1, c)
+        near = [gather_third(pos_sb[0], "near0")]
         first_result = sbuf_tile("first_result", V)
-        for u in range(2):
-            cols = slice(u * UNIT, (u + 1) * UNIT)
-            mean(u, 0, total0["tile"][:, cols], first_result[:, cols])
+        mean(0, 0, total0["tile"], first_result[:, :UNIT])
+        below0 = sbuf_tile("below0", UNIT, "clipped0_1")
+        nc.vector.tensor_tensor(below0, near[0], high, ALU.min)
+        gather_centre(2)
+        t2 = group("turned2", 2 * UNIT, 5, 6)
+        turn_shared(t2, 2, 0, minus_centre(2))
+        inside0 = sbuf_tile("inside0", UNIT)
+        nc.vector.tensor_tensor(inside0, below0, low, ALU.max)
+        mean(1, 0, total1["tile"], first_result[:, UNIT:])
         nc.sync.dma_start(out[0:P, :], first_result)
-        total2 = group("total2", UNIT, 7, 6)
-        last_second, last_third = pair("pulls3", "clipped0_0")
-        gather_plain("scalar", 3, 1, dst=last_second)
-        t3b = [group(f"third{c}", P, (3, 4)[c], 2) for c in range(chunks)]
-        turn_chunks(t3b, 0, minus_centre(3))
-        clip_back(2, 0, t2[0]["tile"], "clipped2_0", total2, 0)
-        turn_chunks(t3, 1, last_second)
-        got = clip_back(2, 1, t2[1]["tile"], "clipped2_1", total2, 1)
-        gather_plain("scalar", 3, 2, dst=last_third)
-        total3 = [group(f"total3_{c}", P, (0, 1)[c], 3) for c in range(chunks)]
-        clip_back(3, 0, t3[0]["tile"], "clipped3_0", total3[0], 0)
-        turn_chunks(t3b, 0, last_third)
-        clip_back(3, 1, t3[1]["tile"], "clipped3_1", total3[1], 0)
+        turn_shared(t2, 2, 0, gather_plain("scalar", 2, 0))
+        t2b = group("third2", UNIT, 7, 4)
+        turn_shared(t2b, 1, 0, minus_centre(2))
+        g22, below1 = pair("held", "clipped1_1")
+        turn_shared(t2, 2, 1, gather_pull(2, 2, dst=g22))
+        near.append(gather_third(pos_sb[1], "near1"))
+        nc.vector.tensor_tensor(below1, near[1], high, ALU.min)
+        turn_shared(t2b, 1, 0, gather_plain("scalar", 2, 1))
+        inside1 = sbuf_tile("inside1", UNIT)
+        nc.vector.tensor_tensor(inside1, below1, low, ALU.max)
+        near.append(gather_third(pos_sb[2], "near2"))
+        total2 = group("total2", UNIT, 3, 6)
+        for c in range(chunks):
+            clip_back(2, c, t2["tile"][:, c * UNIT : (c + 1) * UNIT], f"clipped2_{c}", total2, c)
+        for c in range(chunks):
+            got = clip_back(2, c, part(t2b["tile"], c), f"clipped2b_{c}", total2, c)
+        two, below2 = pair("last_held", "clipped2_0")
+        inside2 = sbuf_tile("inside2", UNIT)
+        last_result = sbuf_tile("last_result", UNIT)
+        nc.vector.tensor_tensor(below2, near[2], high, ALU.min)
+        nc.vector.tensor_tensor(two, inside0, inside1, ALU.add)
+        nc.vector.tensor_tensor(inside2, below2, low, ALU.max)
         finish(2, 0, total2["tile"])
-        for c in range(chunks):
-            clip_back(3, c, t3b[c]["tile"], f"clipped3b_{c}", total3[c], 0)
-        for c in range(chunks):
-            finish(3, c * P, total3[c]["tile"])
+        nc.vector.tensor_tensor(last_result, two, inside2, ALU.add)
+        nc.sync.dma_start(out[P:, V - UNIT :], last_result)

@@ -143,6 +143,7 @@ def tile_picked_huber_none_e_kernel(
         def bring_out(b, h, cols, acc, engine):
             copy_on(engine, y[b][:, h * HALF + cols.start : h * HALF + cols.stop], acc[:])
 
+        early = slice(0, HALF // 2)
         for bank, (h, first, width, engine) in enumerate(FIRST_BLOCK_STEPS):
             cols = slice(first, first + width)
             nc.vector.quantize_mx(
@@ -151,8 +152,10 @@ def tile_picked_huber_none_e_kernel(
                 in_=picked[h][:, cols, :].rearrange("p j t -> p (j t)"),
             )
             bring_out(0, h, cols, product(0, h, cols, bank), engine)
-        whole = slice(0, HALF)
-        second = [product(1, h, whole, SECOND_BLOCK_BANK + h) for h in range(2)]
+            if bank == 1:
+                bring_out(1, 0, early, product(1, 0, early, 6), "scalar")
+        rest = [slice(HALF // 2, HALF), slice(0, HALF)]
+        second = [product(1, h, rest[h], SECOND_BLOCK_BANK + h) for h in range(2)]
 
         def turn(dst, src, start, stop):
             nc.tensor.matmul(dst, src, ident[:], start=start, stop=stop, is_transpose=True)
@@ -244,7 +247,7 @@ def tile_picked_huber_none_e_kernel(
                 turn_into(g, pulls * c + d, part(src, c))
 
         t0 = turned(0, (0, 1), 3, 1)
-        t1 = turned(1, (2, 5), 3, 2)
+        t1 = turned(1, (2, 5), 3, 1)
         total0 = group("total0", UNIT, 6, 6)
         total1 = group("total1", UNIT, 7, 6)
         last = len(units) - 1
@@ -262,13 +265,12 @@ def tile_picked_huber_none_e_kernel(
         turn_chunks(t0, 1, gather_pull(0, 1))
         gather_centre(1)
         turn_chunks(t0, 2, gather_pull(0, 2))
-        for d in range(2):
-            turn_chunks(t1, d, minus_centre(1))
+        turn_chunks(t1, 0, minus_centre(1))
         for h in range(2):
-            bring_out(1, h, whole, second[h], "scalar")
+            bring_out(1, h, rest[h], second[h], "scalar")
         turn_chunks(t1, 2, gather_pull(1, 2))
-        for d in range(2):
-            turn_chunks(t1, d, gather_plain("scalar", 1, d))
+        turn_chunks(t1, 0, gather_plain("scalar", 1, 0))
+        turn_chunks(t1, 1, gather_pull(1, 1))
         for c in range(chunks):
             clip_back(0, c, t0[c]["tile"], f"clipped0_{c}", total0, c)
         centre = gather_third(cen_sb, "centre")
@@ -278,40 +280,47 @@ def tile_picked_huber_none_e_kernel(
         nc.gpsimd.tensor_tensor(low, centre, reach[:], ALU.subtract)
         for c in range(chunks):
             got1 = clip_back(1, c, t1[c]["tile"], f"clipped1_{c}", total1, c)
-        near = [gather_third(pos_sb[0], "near0")]
+        near = [gather_third(pos_sb[d], f"near{d}") for d in range(2)]
+        below = list(pair("below", "gathered1_1"))
+        inside = [sbuf_tile(f"inside{d}", UNIT) for d in range(D)]
+        for d in range(2):
+            nc.vector.tensor_tensor(below[d], near[d], high, ALU.min)
         first_result = sbuf_tile("first_result", V)
         mean(0, 0, total0["tile"], first_result[:, :UNIT])
-        below0 = sbuf_tile("below0", UNIT, "clipped0_1")
-        nc.vector.tensor_tensor(below0, near[0], high, ALU.min)
         gather_centre(2)
-        t2 = group("turned2", 2 * UNIT, 5, 6)
-        turn_shared(t2, 2, 0, minus_centre(2))
-        inside0 = sbuf_tile("inside0", UNIT)
-        nc.vector.tensor_tensor(inside0, below0, low, ALU.max)
+        t2 = group("turned2", 2 * UNIT, 5, 8)
+        for d in range(2):
+            turn_shared(t2, 2, d, minus_centre(2))
+        for d in range(2):
+            nc.vector.tensor_tensor(inside[d], below[d], low, ALU.max)
         mean(1, 0, total1["tile"], first_result[:, UNIT:])
         nc.sync.dma_start(out[0:P, :], first_result)
-        turn_shared(t2, 2, 0, gather_plain("scalar", 2, 0))
-        t2b = group("third2", UNIT, 7, 4)
-        turn_shared(t2b, 1, 0, minus_centre(2))
-        g22, below1 = pair("held", "clipped1_1")
-        turn_shared(t2, 2, 1, gather_pull(2, 2, dst=g22))
-        near.append(gather_third(pos_sb[1], "near1"))
-        nc.vector.tensor_tensor(below1, near[1], high, ALU.min)
-        turn_shared(t2b, 1, 0, gather_plain("scalar", 2, 1))
-        inside1 = sbuf_tile("inside1", UNIT)
-        nc.vector.tensor_tensor(inside1, below1, low, ALU.max)
+        for d in range(2):
+            turn_shared(t2, 2, d, gather_plain("scalar", 2, d))
+        t2b = [group(f"third2_{c}", P, (7, 6)[c], 2) for c in range(chunks)]
+        turn_chunks(t2b, 0, minus_centre(2))
+        two = sbuf_tile("two", UNIT)
+        nc.gpsimd.tensor_tensor(two, inside[0], inside[1], ALU.add)
         near.append(gather_third(pos_sb[2], "near2"))
-        total2 = group("total2", UNIT, 3, 6)
+        total2 = [group(f"total2_{c}", P, (3, 4)[c], 3) for c in range(chunks)]
         for c in range(chunks):
-            clip_back(2, c, t2["tile"][:, c * UNIT : (c + 1) * UNIT], f"clipped2_{c}", total2, c)
+            clip_back(2, c, t2["tile"][:, c * UNIT : (c + 1) * UNIT], f"clipped2_{c}", total2[c], 0)
+        b, v0 = units[2]
         for c in range(chunks):
-            got = clip_back(2, c, part(t2b["tile"], c), f"clipped2b_{c}", total2, c)
-        two, below2 = pair("last_held", "clipped2_0")
-        inside2 = sbuf_tile("inside2", UNIT)
+            piece = sbuf_tile(f"piece{c}", P)
+            nc.scalar.activation(piece, y[b][:].indirect(entries(pos_sb[2], v0 + c * P, P)), COPY)
+            turn_into(t2b[c], 0, piece)
+        below.append(sbuf_tile("below2", UNIT, "gathered2_1"))
         last_result = sbuf_tile("last_result", UNIT)
-        nc.vector.tensor_tensor(below2, near[2], high, ALU.min)
-        nc.vector.tensor_tensor(two, inside0, inside1, ALU.add)
-        nc.vector.tensor_tensor(inside2, below2, low, ALU.max)
-        finish(2, 0, total2["tile"])
-        nc.vector.tensor_tensor(last_result, two, inside2, ALU.add)
+        for c in range(chunks):
+            nc.vector.tensor_tensor(part(below[2], c), part(near[2], c), part(high, c), ALU.min)
+        for c in range(chunks):
+            nc.vector.tensor_tensor(part(inside[2], c), part(below[2], c), part(low, c), ALU.max)
+        clip_back(2, 0, t2b[0]["tile"], "clipped2b_0", total2[0], 0)
+        nc.vector.tensor_tensor(last_result, two, inside[2], ALU.add)
         nc.sync.dma_start(out[P:, V - UNIT :], last_result)
+        clip_back(2, 1, t2b[1]["tile"], "clipped2b_1", total2[1], 0)
+        result2 = sbuf_tile("result2", UNIT)
+        for c in range(chunks):
+            mean(2, c * P, total2[c]["tile"], part(result2, c))
+        nc.sync.dma_start(out[P:, :UNIT], result2)

@@ -21,26 +21,10 @@ P = 128
 PACK = 4
 LAST = PACK - 1
 HALF = S // 2
+QUARTER = S // 4
 D = 3
 PER_COLUMN = 16
 QUADRANT = 32
-
-LAST_PIECES = [
-    (1024, "scalar"),
-    (1024, "scalar"),
-    (1024, "scalar"),
-    (640, "vector"),
-    (256, "vector"),
-    (128, "scalar"),
-]
-FIRST_BLOCK_STEPS = [
-    (0, 0, 256, "scalar"),
-    (0, 256, 256, "scalar"),
-    (1, 0, 256, "vector"),
-    (1, 256, 128, "scalar"),
-    (1, 384, 128, "vector"),
-]
-SECOND_BLOCK_BANK = len(FIRST_BLOCK_STEPS) - 2
 UNIT = 256
 
 
@@ -52,6 +36,9 @@ def tile_picked_huber_none_e_kernel(
         keep = ctx.enter_context(tc.tile_pool(name="keep", bufs=1))
         psum = ctx.enter_context(tc.psum_pool(name="psum", bufs=1))
 
+        def sbuf(name, shape, dtype=F32, over=None):
+            return keep.tile([P] + shape, dtype, name=name, tag=over or name, align_bytes=64)
+
         def load_list(src, name):
             tile = keep.tile(list(src.shape), U16, name=name)
             nc.sync.dma_start(tile[:], src)
@@ -60,75 +47,63 @@ def tile_picked_huber_none_e_kernel(
         def entries(list_tile, first, count):
             return list_tile[:, first // PER_COLUMN : (first + count) // PER_COLUMN]
 
-        def copy_on(engine, dst, src):
-            if engine == "vector":
-                nc.vector.tensor_copy(dst, src)
-            else:
-                nc.scalar.copy(dst, src)
-
-        def bank_tile(width, name, bank):
+        def bank_tile(name, width, bank):
             return psum.tile([P, width], F32, name=name, tag=f"bank{bank}")
 
-        def part(tile, i):
-            return tile[:, i * P : (i + 1) * P]
+        def part(ap, i, width=P):
+            return ap[:, i * width : (i + 1) * width]
 
-        w_scales = keep.tile([P, N], U8, name="w_scales", align_bytes=64)
+        w_scales = sbuf("w_scales", [N], U8)
         nc.vector.memset(w_scales[:].bitcast(I32), 0)
-        ident = keep.tile([P, P], F32, name="ident")
+        ident = sbuf("ident", [P])
         make_identity(nc, ident[:])
 
         rows = xT.rearrange("(p t) c -> p t c", t=PACK)
-        planes = [keep.tile([P, T], F32, name=f"plane{t}") for t in range(PACK)]
+        planes = [sbuf(f"plane{t}", [T]) for t in range(PACK)]
         nc.sync.dma_start(planes[0][:], rows[:, 0, :])
         offs_sb = load_list(offs, "offs_sb")
-        for t in range(1, LAST):
+        for t in range(1, PACK):
             nc.sync.dma_start(planes[t][:], rows[:, t, :])
-        pieces = []
-        first = 0
-        for width, engine in LAST_PIECES:
-            cols = slice(first, first + width)
-            nc.sync.dma_start(planes[LAST][:, cols], rows[:, LAST, cols])
-            pieces.append((cols, engine))
-            first += width
-        cen_sb = load_list(cen, "cen_sb")
-        pos_sb = [load_list(pos1, "pos0_sb")]
-        w_words = keep.tile([P, 2 * N], U8, name="w_words", align_bytes=64)
-        nc.sync.dma_start(w_words[:], w1_words[0])
         for q in range(P // QUADRANT):
             nc.sync.dma_start(
                 w_scales[QUADRANT * q : QUADRANT * q + 4, :].bitcast(I32),
                 w1_scales[0, 4 * q : 4 * q + 4, :].bitcast(I32),
             )
-        far = keep.tile([P, UNIT], F32, name="far")
-        nc.sync.dma_start(far[:], bound[:, V - UNIT :])
-        pos_sb.append(load_list(pos2, "pos1_sb"))
-        pos_sb.append(load_list(pos3, "pos2_sb"))
-
-        upper = keep.tile([P, V // P], F32, name="upper")
-        lower = keep.tile([P, V // P], F32, name="lower")
+        upper = sbuf("upper", [V // P])
         with nc.allow_non_contiguous_dma(reason="512 bounds, one target a partition"):
             nc.sync.dma_start(upper[:], bound[0].rearrange("(c p) -> p c", p=P))
-        nc.scalar.activation(lower[:], upper[:], COPY, scale=-1.0)
+        cen_sb = load_list(cen, "cen_sb")
+        w_words = sbuf("w_words", [2 * N], U8)
+        nc.sync.dma_start(w_words[:], w1_words[0])
+        pos_sb = [load_list(src, f"pos{d}_sb") for d, src in enumerate((pos1, pos2, pos3))]
+        far = sbuf("far", [UNIT])
+        nc.sync.dma_start(far[:], bound[:, V - UNIT :])
 
-        picked = [
-            keep.tile([P, HALF, PACK], BF16, name=f"picked{h}", align_bytes=64) for h in range(2)
-        ]
-        halves = [entries(offs_sb, h * HALF, HALF) for h in range(2)]
-        for t in range(LAST):
-            for h in range(2):
-                nc.vector.tensor_copy(picked[h][:, :, t], planes[t][:].indirect(halves[h]))
-        rounded = keep.tile([P, T], BF16, name="rounded")
-        for cols, engine in pieces:
-            copy_on(engine, rounded[:, cols], planes[LAST][:, cols])
-        nc.vector.tensor_copy(picked[0][:, :, LAST], planes[LAST][:].indirect(halves[0]))
-        nc.scalar.activation(picked[1][:, :, LAST], rounded[:].indirect(halves[1]), COPY)
+        first_half = sbuf("first_half", [HALF, PACK], BF16)
+        quarters = [sbuf(f"quarter{i}", [QUARTER, PACK], BF16) for i in range(2)]
 
-        codes = [keep.tile([P, HALF], U32, name=f"codes{h}", align_bytes=64) for h in range(2)]
-        scales = [keep.tile([P, HALF], U8, name=f"scales{h}", align_bytes=64) for h in range(2)]
-        y = [keep.tile([P, S], F32, name=f"y{b}") for b in range(N // P)]
+        def fetch(name, t, first, count):
+            tile = sbuf(name, [count], BF16)
+            nc.scalar.activation(tile[:], planes[t][:].indirect(entries(offs_sb, first, count)), COPY)
+            return tile
+
+        for t in range(PACK):
+            nc.vector.tensor_copy(first_half[:, :, t], planes[t][:].indirect(entries(offs_sb, 0, HALF)))
+            if t < LAST:
+                plain = fetch(f"plain{t}", t, HALF, HALF)
+                for i in range(2):
+                    nc.scalar.copy(quarters[i][:, :, t], part(plain, i, QUARTER))
+        plain = [fetch(f"plain{LAST}_{i}", LAST, HALF + i * QUARTER, QUARTER) for i in (1, 0)]
+        nc.scalar.copy(quarters[0][:, :, LAST], plain[1][:])
+        nc.vector.tensor_copy(quarters[1][:, :P, LAST], plain[0][:, :P])
+        nc.scalar.copy(quarters[1][:, P:, LAST], plain[0][:, P:])
+
+        codes = [sbuf("codes0", [HALF], U32), sbuf("codes1", [HALF], U32)]
+        scales = [sbuf(f"scales{h}", [HALF], U8) for h in range(2)]
+        y = [sbuf(f"y{b}", [S]) for b in range(N // P)]
 
         def product(b, h, cols, bank):
-            acc = bank_tile(cols.stop - cols.start, "acc", bank)
+            acc = bank_tile("acc", cols.stop - cols.start, bank)
             nc.tensor.matmul_mx(
                 out=acc[:],
                 lhsT=w_words[:, 2 * P * b : 2 * P * (b + 1)].bitcast(FP4X4),
@@ -141,186 +116,156 @@ def tile_picked_huber_none_e_kernel(
             return acc
 
         def bring_out(b, h, cols, acc, engine):
-            copy_on(engine, y[b][:, h * HALF + cols.start : h * HALF + cols.stop], acc[:])
+            dst = y[b][:, h * HALF + cols.start : h * HALF + cols.stop]
+            if engine == "vector":
+                nc.vector.tensor_copy(dst, acc[:])
+            else:
+                nc.scalar.copy(dst, acc[:])
 
-        early = slice(0, HALF // 2)
-        for bank, (h, first, width, engine) in enumerate(FIRST_BLOCK_STEPS):
-            cols = slice(first, first + width)
+        steps = [
+            (0, 0, first_half[:, :QUARTER, :], "scalar"),
+            (0, QUARTER, first_half[:, QUARTER:, :], "scalar"),
+            (1, 0, quarters[0][:], "vector"),
+            (1, QUARTER, quarters[1][:, :P, :], "scalar"),
+            (1, QUARTER + P, quarters[1][:, P:, :], "vector"),
+        ]
+        for bank, (h, first, src, engine) in enumerate(steps):
+            cols = slice(first, first + src.shape[1])
             nc.vector.quantize_mx(
                 out=codes[h][:, cols].bitcast(FP8X4),
                 scales=scales[h][:, cols],
-                in_=picked[h][:, cols, :].rearrange("p j t -> p (j t)"),
+                in_=src.rearrange("p j t -> p (j t)"),
             )
             bring_out(0, h, cols, product(0, h, cols, bank), engine)
             if bank == 1:
-                bring_out(1, 0, early, product(1, 0, early, 6), "scalar")
-        rest = [slice(HALF // 2, HALF), slice(0, HALF)]
-        second = [product(1, h, rest[h], SECOND_BLOCK_BANK + h) for h in range(2)]
+                early = slice(0, QUARTER)
+                bring_out(1, 0, early, product(1, 0, early, 7), "scalar")
+        later = [slice(QUARTER, HALF), slice(0, HALF)]
+        second = [product(1, h, later[h], 2 + h) for h in range(2)]
 
-        def turn(dst, src, start, stop):
-            nc.tensor.matmul(dst, src, ident[:], start=start, stop=stop, is_transpose=True)
+        scaled = sbuf("scaled", [UNIT + V // P], over="quarter1")
+        reach, lower = scaled[:, :UNIT], scaled[:, UNIT:]
+        nc.gpsimd.tensor_scalar(reach, far[:], 1.0 / D, 0.0, ALU.mult, ALU.add)
+        nc.gpsimd.tensor_scalar(lower, upper[:], -1.0, 0.0, ALU.mult, ALU.add)
 
-        units = [(b, v0) for b in range(N // P) for v0 in range(0, V, UNIT)]
-        chunks = UNIT // P
+        def picked_by(list_tile, b, first, count=UNIT):
+            return y[b][:].indirect(entries(list_tile, first, count))
 
-        def sbuf_tile(name, width, after=None):
-            return keep.tile([P, width], F32, name=name, tag=after or name)[:]
-
-        def picked_by(list_tile, u):
-            b, v0 = units[u]
-            return y[b][:].indirect(entries(list_tile, v0, UNIT))
-
-        negated = {}
-
-        def minus_centre(u):
-            return negated[u]
-
-        def gather_centre(u, dst=None):
-            negated[u] = sbuf_tile(f"negated{u}", UNIT) if dst is None else dst
-            nc.scalar.activation(minus_centre(u), picked_by(cen_sb, u), COPY, scale=-1.0)
+        def fetch_scalar(name, list_tile, b, first, count=UNIT, scale=1.0):
+            dst = sbuf(name, [count])
+            nc.scalar.activation(dst[:], picked_by(list_tile, b, first, count), COPY, scale=scale)
+            return dst
 
         def group(name, width, bank, count):
-            return {"tile": bank_tile(width, name, bank)[:], "left": count, "count": count}
+            return {"tile": bank_tile(name, width, bank), "left": count, "count": count}
 
-        def turn_into(g, i, src):
+        def turn(g, slot, src):
             g["left"] -= 1
-            turn(part(g["tile"], i), src, g["left"] == g["count"] - 1, g["left"] == 0)
-
-        def gather_plain(engine, u, d, after=None, dst=None):
-            if dst is None:
-                dst = sbuf_tile(f"gathered{u}_{d}", UNIT, after)
-            if engine == "vector":
-                nc.vector.tensor_copy(dst, picked_by(pos_sb[d], u))
-            else:
-                nc.scalar.activation(dst, picked_by(pos_sb[d], u), COPY)
-            return dst
-
-        def gather_pull(u, d, after=None, dst=None):
-            if dst is None:
-                dst = sbuf_tile(f"gathered{u}_{d}", UNIT, after)
-            nc.vector.tensor_tensor(dst, picked_by(pos_sb[d], u), minus_centre(u), ALU.add)
-            return dst
-
-        def turn_chunks(groups, i, src):
-            for c in range(chunks):
-                turn_into(groups[c], i, part(src, c))
-
-        def clip(u, c, source, name, engine=nc.vector):
-            col = slice(units[u][1] // P + c, units[u][1] // P + c + 1)
-            clipped = sbuf_tile(name, source.shape[1])
-            engine.tensor_scalar(clipped, source, upper[:, col], lower[:, col], ALU.min, ALU.max)
-            return clipped
-
-        def clip_back(u, c, source, name, total, i, engine=nc.vector):
-            clipped = clip(u, c, source, name, engine)
-            for d in range(source.shape[1] // P):
-                turn_into(total, i, part(clipped, d))
-            return clipped
-
-        def empty(source, name):
-            dst = sbuf_tile(name, source.shape[1])
-            nc.scalar.copy(dst, source)
-            return dst
-
-        def mean(u, first, sums, result):
-            cols = slice(first, first + sums.shape[1])
-            nc.vector.scalar_tensor_tensor(
-                result, sums, 1.0 / D, negated[u][:, cols], ALU.mult, ALU.subtract
+            nc.tensor.matmul(
+                part(g["tile"], slot), src, ident[:],
+                start=g["left"] == g["count"] - 1, stop=g["left"] == 0, is_transpose=True,
             )
 
-        def finish(u, first, sums):
-            b, v0 = units[u]
-            width = sums.shape[1]
-            result = sbuf_tile(f"result{u}_{first}", width)
-            mean(u, first, sums, result)
-            nc.sync.dma_start(out[b * P : (b + 1) * P, v0 + first : v0 + first + width], result)
-
-        def pair(name, after):
-            tile = sbuf_tile(name, 2 * UNIT, after)
-            return tile[:, :UNIT], tile[:, UNIT:]
-
-        def turned(u, banks, pulls, plain):
-            return [group(f"turned{u}_{c}", pulls * P, banks[c], pulls + plain) for c in range(chunks)]
-
-        def turn_shared(g, pulls, d, src):
-            for c in range(chunks):
-                turn_into(g, pulls * c + d, part(src, c))
-
-        t0 = turned(0, (0, 1), 3, 1)
-        t1 = turned(1, (2, 5), 3, 1)
-        total0 = group("total0", UNIT, 6, 6)
-        total1 = group("total1", UNIT, 7, 6)
-        last = len(units) - 1
-        reach = keep.tile([P, UNIT], F32, name="reach", tag="picked1", align_bytes=64)
-        nc.gpsimd.tensor_scalar(reach[:], far[:], 1.0 / D, 0.0, ALU.mult, ALU.add)
-
-        def gather_third(list_tile, name):
-            dst = sbuf_tile(name, UNIT)
-            nc.scalar.activation(dst, picked_by(list_tile, last), COPY, scale=1.0 / D)
+        def clip(name, chunk, source):
+            dst = sbuf(name, [source.shape[1]])
+            col = slice(chunk, chunk + 1)
+            nc.vector.tensor_scalar(dst[:], source, upper[:, col], lower[:, col], ALU.min, ALU.max)
             return dst
 
-        gather_centre(0)
-        turn_chunks(t0, 0, gather_plain("vector", 0, 0))
-        turn_chunks(t0, 0, minus_centre(0))
-        turn_chunks(t0, 1, gather_pull(0, 1))
-        gather_centre(1)
-        turn_chunks(t0, 2, gather_pull(0, 2))
-        turn_chunks(t1, 0, minus_centre(1))
+        def turn_back(g, slot, clipped):
+            for d in range(clipped.shape[1] // P):
+                turn(g, slot, part(clipped, d))
+
+        def mean(dst, sums, negated):
+            nc.vector.scalar_tensor_tensor(dst, sums, 1.0 / D, negated, ALU.mult, ALU.subtract)
+
+        t0 = [group(f"t0_{c}", D * P, c, D + 1) for c in range(2)]
+        neg0 = fetch_scalar("neg0", cen_sb, 0, 0, scale=-1.0)
+        pull = sbuf("pull00", [UNIT])
+        nc.vector.tensor_copy(pull[:], picked_by(pos_sb[0], 0, 0))
+        for c in range(2):
+            turn(t0[c], 0, part(pull, c))
+            turn(t0[c], 0, part(neg0, c))
+        for d in range(1, D):
+            pull = sbuf(f"pull0{d}", [UNIT])
+            nc.vector.tensor_tensor(pull[:], picked_by(pos_sb[d], 0, 0), neg0[:], ALU.add)
+            for c in range(2):
+                turn(t0[c], d, part(pull, c))
+        centre = fetch_scalar("centre", cen_sb, 0, UNIT)
         for h in range(2):
-            bring_out(1, h, rest[h], second[h], "scalar")
-        turn_chunks(t1, 2, gather_pull(1, 2))
-        turn_chunks(t1, 0, gather_plain("scalar", 1, 0))
-        turn_chunks(t1, 1, gather_pull(1, 1))
-        for c in range(chunks):
-            clip_back(0, c, t0[c]["tile"], f"clipped0_{c}", total0, c)
-        centre = gather_third(cen_sb, "centre")
-        high = sbuf_tile("high", UNIT)
-        low = sbuf_tile("low", UNIT)
-        nc.gpsimd.tensor_tensor(high, centre, reach[:], ALU.add)
-        nc.gpsimd.tensor_tensor(low, centre, reach[:], ALU.subtract)
-        for c in range(chunks):
-            got1 = clip_back(1, c, t1[c]["tile"], f"clipped1_{c}", total1, c)
-        near = [gather_third(pos_sb[d], f"near{d}") for d in range(2)]
-        below = list(pair("below", "gathered1_1"))
-        inside = [sbuf_tile(f"inside{d}", UNIT) for d in range(D)]
+            bring_out(1, h, later[h], second[h], "scalar")
+        near = sbuf("near", [D, UNIT], over="pull00")
+        for d in range(D):
+            nc.vector.tensor_copy(near[:, d, :], picked_by(pos_sb[d], 0, UNIT))
+        limits = sbuf("limits", [2 * UNIT], over="pull01")
+        high, third = part(limits, 0, UNIT), part(limits, 1, UNIT)
+        low = sbuf("low", [UNIT])
+        nc.gpsimd.tensor_tensor(high, centre[:], far[:], ALU.add)
+        nc.gpsimd.tensor_scalar(third, centre[:], 1.0 / D, 0.0, ALU.mult, ALU.add)
+        nc.gpsimd.tensor_tensor(low[:], third, reach, ALU.subtract)
+
+        neg2 = fetch_scalar("neg2", cen_sb, 1, 0, scale=-1.0)
+        neg3 = fetch_scalar("neg3", cen_sb, 1, UNIT, scale=-1.0)
+        t2 = [group("t2_0", (D + 1) * P, 5, 3 * D), group("t2_1", D * P, 6, 2 * D)]
+        thirds = group("thirds", 3 * P, 4, 4 + D)
+        for c in range(2):
+            for d in range(D):
+                turn(t2[c], d, part(neg2, c))
+        for c in range(2):
+            turn(thirds, c, part(neg3, c))
+        pulls2 = [fetch_scalar(f"pull2{d}", pos_sb[d], 1, 0) for d in range(D)]
+        pulls3 = [fetch_scalar(f"pull3{d}", pos_sb[d], 1, UNIT) for d in range(2)]
+        pieces = [fetch_scalar(f"piece{c}", pos_sb[2], 1, UNIT + c * P, P) for c in range(2)]
+        for c in range(2):
+            turn(t2[c], 0, part(pulls2[0], c))
+        turn_back(t2[0], D, clip("clipped0", 0, t0[0]["tile"][:]))
+        pairs = [group("pair0", D * P, 0, 4 + D)]
         for d in range(2):
-            nc.vector.tensor_tensor(below[d], near[d], high, ALU.min)
-        first_result = sbuf_tile("first_result", V)
-        mean(0, 0, total0["tile"], first_result[:, :UNIT])
-        gather_centre(2)
-        t2 = group("turned2", 2 * UNIT, 5, 8)
+            turn(pairs[0], d, part(neg3, 0))
+        for d in range(1, D):
+            for c in range(2):
+                turn(t2[c], d, part(pulls2[d], c))
+
+        def thrice(ap):
+            return ap.unsqueeze(1).to_broadcast([P, D, UNIT])
+
+        below = sbuf("below", [D, UNIT], over="pull02")
+        nc.vector.tensor_tensor(below[:], near[:], thrice(high), ALU.min)
+        turn_back(pairs[0], 2, clip("clipped1", 1, t0[1]["tile"][:]))
+        pairs.append(group("pair1", 2 * P, 1, 4))
         for d in range(2):
-            turn_shared(t2, 2, d, minus_centre(2))
+            turn(pairs[1], d, part(neg3, 1))
         for d in range(2):
-            nc.vector.tensor_tensor(inside[d], below[d], low, ALU.max)
-        mean(1, 0, total1["tile"], first_result[:, UNIT:])
-        nc.sync.dma_start(out[0:P, :], first_result)
-        for d in range(2):
-            turn_shared(t2, 2, d, gather_plain("scalar", 2, d))
-        t2b = [group(f"third2_{c}", P, (7, 6)[c], 2) for c in range(chunks)]
-        turn_chunks(t2b, 0, minus_centre(2))
-        two = sbuf_tile("two", UNIT)
-        nc.gpsimd.tensor_tensor(two, inside[0], inside[1], ALU.add)
-        near.append(gather_third(pos_sb[2], "near2"))
-        total2 = [group(f"total2_{c}", P, (3, 4)[c], 3) for c in range(chunks)]
-        for c in range(chunks):
-            clip_back(2, c, t2["tile"][:, c * UNIT : (c + 1) * UNIT], f"clipped2_{c}", total2[c], 0)
-        b, v0 = units[2]
-        for c in range(chunks):
-            piece = sbuf_tile(f"piece{c}", P)
-            nc.scalar.activation(piece, y[b][:].indirect(entries(pos_sb[2], v0 + c * P, P)), COPY)
-            turn_into(t2b[c], 0, piece)
-        below.append(sbuf_tile("below2", UNIT, "gathered2_1"))
-        last_result = sbuf_tile("last_result", UNIT)
-        for c in range(chunks):
-            nc.vector.tensor_tensor(part(below[2], c), part(near[2], c), part(high, c), ALU.min)
-        for c in range(chunks):
-            nc.vector.tensor_tensor(part(inside[2], c), part(below[2], c), part(low, c), ALU.max)
-        clip_back(2, 0, t2b[0]["tile"], "clipped2b_0", total2[0], 0)
-        nc.vector.tensor_tensor(last_result, two, inside[2], ALU.add)
-        nc.sync.dma_start(out[P:, V - UNIT :], last_result)
-        clip_back(2, 1, t2b[1]["tile"], "clipped2b_1", total2[1], 0)
-        result2 = sbuf_tile("result2", UNIT)
-        for c in range(chunks):
-            mean(2, c * P, total2[c]["tile"], part(result2, c))
-        nc.sync.dma_start(out[P:, :UNIT], result2)
+            for c in range(2):
+                turn(pairs[c], d, part(pulls3[d], c))
+        inside = sbuf("inside", [D, UNIT])
+        nc.vector.scalar_tensor_tensor(inside[:], below[:], 1.0 / D, thrice(low[:]), ALU.mult, ALU.max)
+        turn_back(thirds, 2, clip("clipped4", 0, t2[0]["tile"][:, : D * P]))
+        for c in range(2):
+            turn(thirds, c, pieces[c][:])
+        two = sbuf("two", [UNIT])
+        result1 = sbuf("result1", [UNIT])
+        nc.gpsimd.tensor_tensor(two[:], inside[:, 0, :], inside[:, 1, :], ALU.add)
+        nc.gpsimd.tensor_tensor(result1[:], two[:], inside[:, 2, :], ALU.add)
+        nc.sync.dma_start(out[:P, UNIT:], result1[:])
+        sum2b = group("sum2b", P, 7, D)
+        turn_back(sum2b, 0, clip("clipped5", 1, t2[1]["tile"][:, : D * P]))
+        sum3 = [group(f"sum3_{c}", P, 2 + c, D) for c in range(2)]
+        for c in range(2):
+            turn_back(sum3[c], 0, clip(f"pair{c}", 2 + c, pairs[c]["tile"][:, :UNIT]))
+        moved = sbuf("moved", [UNIT])
+        for c, sums in enumerate((part(t2[0]["tile"], D), part(pairs[0]["tile"], 2))):
+            nc.scalar.activation(part(moved, c), sums, COPY, scale=1.0 / D)
+        result0 = sbuf("result0", [UNIT])
+        nc.gpsimd.tensor_tensor(result0[:], moved[:], neg0[:], ALU.subtract)
+        nc.sync.dma_start(out[:P, :UNIT], result0[:])
+        for c in range(2):
+            turn_back(sum3[c], 0, clip(f"last{c}", 2 + c, part(thirds["tile"], c)))
+        result2 = sbuf("result2", [UNIT])
+        mean(part(result2, 0), part(thirds["tile"], 2), part(neg2, 0))
+        mean(part(result2, 1), sum2b["tile"][:], part(neg2, 1))
+        nc.sync.dma_start(out[P:, :UNIT], result2[:])
+        result3 = sbuf("result3", [UNIT])
+        for c in range(2):
+            mean(part(result3, c), sum3[c]["tile"][:], part(neg3, c))
+        nc.sync.dma_start(out[P:, UNIT:], result3[:])

@@ -247,7 +247,8 @@ def tile_picked_huber_none_e_kernel(
         result1 = sbuf("result1", [UNIT])
         nc.gpsimd.tensor_tensor(two[:], inside[:, 0, :], inside[:, 1, :], ALU.add)
         nc.gpsimd.tensor_tensor(result1[:], two[:], inside[:, 2, :], ALU.add)
-        nc.sync.dma_start(out[:P, UNIT:], result1[:])
+        for c in range(2):
+            nc.sync.dma_start(out[:P, UNIT + c * P : UNIT + (c + 1) * P], part(result1, c))
         sum2b = group("sum2b", P, 7, D)
         turn_back(sum2b, 0, clip("clipped5", 1, t2[1]["tile"][:, : D * P]))
         sum3 = [group(f"sum3_{c}", P, 2 + c, D) for c in range(2)]
@@ -258,14 +259,12 @@ def tile_picked_huber_none_e_kernel(
             nc.scalar.activation(part(moved, c), sums, COPY, scale=1.0 / D)
         result0 = sbuf("result0", [UNIT])
         nc.gpsimd.tensor_tensor(result0[:], moved[:], neg0[:], ALU.subtract)
-        nc.sync.dma_start(out[:P, :UNIT], result0[:])
         for c in range(2):
-            turn_back(sum3[c], 0, clip(f"last{c}", 2 + c, part(thirds["tile"], c)))
-        result2 = sbuf("result2", [UNIT])
-        mean(part(result2, 0), part(thirds["tile"], 2), part(neg2, 0))
-        mean(part(result2, 1), sum2b["tile"][:], part(neg2, 1))
-        nc.sync.dma_start(out[P:, :UNIT], result2[:])
-        result3 = sbuf("result3", [UNIT])
+            nc.scalar.dma_start(out[:P, c * P : (c + 1) * P], part(result0, c))
         for c in range(2):
-            mean(part(result3, c), sum3[c]["tile"][:], part(neg3, c))
-        nc.sync.dma_start(out[P:, UNIT:], result3[:])
+            turn_back(sum3[c], 0, clip(f"third{c}", 2 + c, part(thirds["tile"], c)))
+        second_rows = sbuf("second_rows", [V])
+        ends = [part(thirds["tile"], 2), sum2b["tile"][:], sum3[0]["tile"][:], sum3[1]["tile"][:]]
+        for c, src in enumerate(ends):
+            mean(part(second_rows, c), src, part((neg2, neg3)[c // 2], c % 2))
+            nc.sync.dma_start(out[P:, c * P : (c + 1) * P], part(second_rows, c))

@@ -69,15 +69,17 @@ def tile_picked_huber_none_e_kernel(
                 w_scales[QUADRANT * q : QUADRANT * q + 4, :].bitcast(I32),
                 w1_scales[0, 4 * q : 4 * q + 4, :].bitcast(I32),
             )
+        cen_sb = load_list(cen, "cen_sb")
+        pos_sb = [load_list(pos1, "pos0_sb")]
+        w_words = sbuf("w_words", [2 * N], U8)
+        nc.sync.dma_start(w_words[:], w1_words[0])
+        pos_sb.append(load_list(pos2, "pos1_sb"))
+        pos_sb.append(load_list(pos3, "pos2_sb"))
+        far = sbuf("far", [UNIT])
+        nc.sync.dma_start(far[:], bound[:, V - UNIT :])
         upper = sbuf("upper", [V // P])
         with nc.allow_non_contiguous_dma(reason="512 bounds, one target a partition"):
             nc.sync.dma_start(upper[:], bound[0].rearrange("(c p) -> p c", p=P))
-        cen_sb = load_list(cen, "cen_sb")
-        w_words = sbuf("w_words", [2 * N], U8)
-        nc.sync.dma_start(w_words[:], w1_words[0])
-        pos_sb = [load_list(src, f"pos{d}_sb") for d, src in enumerate((pos1, pos2, pos3))]
-        far = sbuf("far", [UNIT])
-        nc.sync.dma_start(far[:], bound[:, V - UNIT :])
 
         first_half = sbuf("first_half", [HALF, PACK], BF16)
         quarters = [sbuf(f"quarter{i}", [QUARTER, PACK], BF16) for i in range(2)]
@@ -93,12 +95,13 @@ def tile_picked_huber_none_e_kernel(
                 plain = fetch(f"plain{t}", t, HALF, HALF)
                 for i in range(2):
                     nc.scalar.copy(quarters[i][:, :, t], part(plain, i, QUARTER))
-        plain = [fetch(f"plain{LAST}_{i}", LAST, HALF + i * QUARTER, QUARTER) for i in (1, 0)]
-        nc.scalar.copy(quarters[0][:, :, LAST], plain[1][:])
-        nc.vector.tensor_copy(quarters[1][:, :P, LAST], plain[0][:, :P])
-        nc.scalar.copy(quarters[1][:, P:, LAST], plain[0][:, P:])
+        eighth = fetch("last0", LAST, HALF, P)
+        others = fetch("last1", LAST, HALF + P, HALF - P)
+        nc.vector.tensor_copy(quarters[0][:, :P, LAST], eighth[:])
+        nc.scalar.copy(quarters[0][:, P:, LAST], others[:, :P])
+        nc.scalar.copy(quarters[1][:, :, LAST], others[:, P:])
 
-        codes = [sbuf("codes0", [HALF], U32), sbuf("codes1", [HALF], U32)]
+        codes = [sbuf("codes0", [HALF], U32, over=f"plane{LAST}"), sbuf("codes1", [HALF], U32)]
         scales = [sbuf(f"scales{h}", [HALF], U8) for h in range(2)]
         y = [sbuf(f"y{b}", [S]) for b in range(N // P)]
 

@@ -207,8 +207,8 @@ def tile_picked_huber_none_e_kernel(
         nc.gpsimd.tensor_scalar(third, centre[:], 1.0 / D, 0.0, ALU.mult, ALU.add)
         nc.gpsimd.tensor_tensor(low[:], third, reach, ALU.subtract)
 
-        neg2 = fetch_scalar("neg2", cen_sb, 1, 0, scale=-1.0)
-        neg3 = fetch_scalar("neg3", cen_sb, 1, UNIT, scale=-1.0)
+        negated = fetch_scalar("negated", cen_sb, 1, 0, V, scale=-1.0)
+        neg2, neg3 = part(negated, 0, UNIT), part(negated, 1, UNIT)
         t2 = [group("t2_0", (D + 1) * P, 5, 3 * D), group("t2_1", D * P, 6, 2 * D)]
         thirds = group("thirds", 3 * P, 4, 4 + D)
         for c in range(2):
@@ -216,15 +216,15 @@ def tile_picked_huber_none_e_kernel(
                 turn(t2[c], d, part(neg2, c))
         for c in range(2):
             turn(thirds, c, part(neg3, c))
+        pairs = [group("pair0", D * P, 2, 4 + D)]
+        for d in range(2):
+            turn(pairs[0], d, part(neg3, 0))
         pulls2 = [fetch_scalar(f"pull2{d}", pos_sb[d], 1, 0) for d in range(D)]
         pulls3 = [fetch_scalar(f"pull3{d}", pos_sb[d], 1, UNIT) for d in range(2)]
         pieces = [fetch_scalar(f"piece{c}", pos_sb[2], 1, UNIT + c * P, P) for c in range(2)]
         for c in range(2):
             turn(t2[c], 0, part(pulls2[0], c))
         turn_back(t2[0], D, clip("clipped0", 0, t0[0]["tile"][:]))
-        pairs = [group("pair0", D * P, 0, 4 + D)]
-        for d in range(2):
-            turn(pairs[0], d, part(neg3, 0))
         for d in range(1, D):
             for c in range(2):
                 turn(t2[c], d, part(pulls2[d], c))
@@ -254,7 +254,7 @@ def tile_picked_huber_none_e_kernel(
             nc.sync.dma_start(out[:P, UNIT + c * P : UNIT + (c + 1) * P], part(result1, c))
         sum2b = group("sum2b", P, 7, D)
         turn_back(sum2b, 0, clip("clipped5", 1, t2[1]["tile"][:, : D * P]))
-        sum3 = [group(f"sum3_{c}", P, 2 + c, D) for c in range(2)]
+        sum3 = [group(f"sum3_{c}", P, 3 * c, D) for c in range(2)]
         for c in range(2):
             turn_back(sum3[c], 0, clip(f"pair{c}", 2 + c, pairs[c]["tile"][:, :UNIT]))
         moved = sbuf("moved", [UNIT])
@@ -269,5 +269,5 @@ def tile_picked_huber_none_e_kernel(
         second_rows = sbuf("second_rows", [V])
         ends = [part(thirds["tile"], 2), sum2b["tile"][:], sum3[0]["tile"][:], sum3[1]["tile"][:]]
         for c, src in enumerate(ends):
-            mean(part(second_rows, c), src, part((neg2, neg3)[c // 2], c % 2))
+            mean(part(second_rows, c), src, part(negated, c))
             nc.sync.dma_start(out[P:, c * P : (c + 1) * P], part(second_rows, c))

@@ -146,10 +146,8 @@ def tile_picked_huber_none_e_kernel(
         later = [slice(QUARTER, HALF), slice(0, HALF)]
         second = [product(1, h, later[h], 2 + h) for h in range(2)]
 
-        scaled = sbuf("scaled", [UNIT + V // P], over="quarter1")
-        reach, lower = scaled[:, :UNIT], scaled[:, UNIT:]
-        nc.gpsimd.tensor_scalar(reach, far[:], 1.0 / D, 0.0, ALU.mult, ALU.add)
-        nc.gpsimd.tensor_scalar(lower, upper[:], -1.0, 0.0, ALU.mult, ALU.add)
+        reach = sbuf("reach", [UNIT], over="quarter1")
+        nc.gpsimd.tensor_scalar(reach[:], far[:], 1.0 / D, 0.0, ALU.mult, ALU.add)
 
         def picked_by(list_tile, b, first, count=UNIT):
             return y[b][:].indirect(entries(list_tile, first, count))
@@ -194,18 +192,17 @@ def tile_picked_huber_none_e_kernel(
             nc.vector.tensor_tensor(pull[:], picked_by(pos_sb[d], 0, 0), neg0[:], ALU.add)
             for c in range(2):
                 turn(t0[c], d, part(pull, c))
-        centre = fetch_scalar("centre", cen_sb, 0, UNIT)
+        centre = fetch_scalar("centre", cen_sb, 0, UNIT, scale=1.0 / D)
         for h in range(2):
             bring_out(1, h, later[h], second[h], "scalar")
         near = sbuf("near", [D, UNIT], over="pull00")
         for d in range(D):
             nc.vector.tensor_copy(near[:, d, :], picked_by(pos_sb[d], 0, UNIT))
-        limits = sbuf("limits", [2 * UNIT], over="pull01")
-        high, third = part(limits, 0, UNIT), part(limits, 1, UNIT)
-        low = sbuf("low", [UNIT])
-        nc.gpsimd.tensor_tensor(high, centre[:], far[:], ALU.add)
-        nc.gpsimd.tensor_scalar(third, centre[:], 1.0 / D, 0.0, ALU.mult, ALU.add)
-        nc.gpsimd.tensor_tensor(low[:], third, reach, ALU.subtract)
+        limits = sbuf("limits", [2 * UNIT + V // P], over="pull01")
+        high, low, lower = part(limits, 0, UNIT), part(limits, 1, UNIT), limits[:, 2 * UNIT :]
+        nc.gpsimd.tensor_scalar(lower, upper[:], -1.0, 0.0, ALU.mult, ALU.add)
+        nc.gpsimd.tensor_tensor(high, centre[:], reach[:], ALU.add)
+        nc.gpsimd.tensor_tensor(low, centre[:], reach[:], ALU.subtract)
 
         negated = fetch_scalar("negated", cen_sb, 1, 0, V, scale=-1.0)
         neg2, neg3 = part(negated, 0, UNIT), part(negated, 1, UNIT)
@@ -233,7 +230,7 @@ def tile_picked_huber_none_e_kernel(
             return ap.unsqueeze(1).to_broadcast([P, D, UNIT])
 
         below = sbuf("below", [D, UNIT], over="pull02")
-        nc.vector.tensor_tensor(below[:], near[:], thrice(high), ALU.min)
+        nc.vector.scalar_tensor_tensor(below[:], near[:], 1.0 / D, thrice(high), ALU.mult, ALU.min)
         turn_back(pairs[0], 2, clip("clipped1", 1, t0[1]["tile"][:]))
         pairs.append(group("pair1", 2 * P, 1, 4))
         for d in range(2):
@@ -242,7 +239,7 @@ def tile_picked_huber_none_e_kernel(
             for c in range(2):
                 turn(pairs[c], d, part(pulls3[d], c))
         inside = sbuf("inside", [D, UNIT])
-        nc.vector.scalar_tensor_tensor(inside[:], below[:], 1.0 / D, thrice(low[:]), ALU.mult, ALU.max)
+        nc.vector.tensor_tensor(inside[:], below[:], thrice(low), ALU.max)
         turn_back(thirds, 2, clip("clipped4", 0, t2[0]["tile"][:, : D * P]))
         for c in range(2):
             turn(thirds, c, pieces[c][:])

@@ -69,14 +69,12 @@ def tile_picked_huber_none_e_kernel(
                 w_scales[QUADRANT * q : QUADRANT * q + 4, :].bitcast(I32),
                 w1_scales[0, 4 * q : 4 * q + 4, :].bitcast(I32),
             )
-        cen_sb = load_list(cen, "cen_sb")
-        pos_sb = [load_list(pos1, "pos0_sb")]
-        w_words = sbuf("w_words", [2 * N], U8)
-        nc.sync.dma_start(w_words[:], w1_words[0])
-        pos_sb.append(load_list(pos2, "pos1_sb"))
-        pos_sb.append(load_list(pos3, "pos2_sb"))
         far = sbuf("far", [UNIT])
         nc.sync.dma_start(far[:], bound[:, V - UNIT :])
+        cen_sb = load_list(cen, "cen_sb")
+        w_words = sbuf("w_words", [2 * N], U8)
+        nc.sync.dma_start(w_words[:], w1_words[0])
+        pos_sb = [load_list(src, f"pos{d}_sb") for d, src in enumerate((pos1, pos2, pos3))]
         upper = sbuf("upper", [V // P])
         with nc.allow_non_contiguous_dma(reason="512 bounds, one target a partition"):
             nc.sync.dma_start(upper[:], bound[0].rearrange("(c p) -> p c", p=P))
@@ -204,8 +202,8 @@ def tile_picked_huber_none_e_kernel(
         nc.gpsimd.tensor_tensor(high, centre[:], reach[:], ALU.add)
         nc.gpsimd.tensor_tensor(low, centre[:], reach[:], ALU.subtract)
 
-        negated = fetch_scalar("negated", cen_sb, 1, 0, V, scale=-1.0)
-        neg2, neg3 = part(negated, 0, UNIT), part(negated, 1, UNIT)
+        neg2 = fetch_scalar("neg2", cen_sb, 1, 0, scale=-1.0)
+        neg3 = fetch_scalar("neg3", cen_sb, 1, UNIT, scale=-1.0)
         t2 = [group("t2_0", (D + 1) * P, 5, 3 * D), group("t2_1", D * P, 6, 2 * D)]
         thirds = group("thirds", 3 * P, 4, 4 + D)
         for c in range(2):
@@ -266,5 +264,5 @@ def tile_picked_huber_none_e_kernel(
         second_rows = sbuf("second_rows", [V])
         ends = [part(thirds["tile"], 2), sum2b["tile"][:], sum3[0]["tile"][:], sum3[1]["tile"][:]]
         for c, src in enumerate(ends):
-            mean(part(second_rows, c), src, part(negated, c))
+            mean(part(second_rows, c), src, part((neg2, neg3)[c // 2], c % 2))
             nc.sync.dma_start(out[P:, c * P : (c + 1) * P], part(second_rows, c))

from contextlib import ExitStack

import concourse.mybir as mybir
from concourse.masks import make_identity

K, T, S, V, N = 512, 4096, 1024, 512, 256
FLOPS = 2 * K * N * S

F32 = mybir.dt.float32
BF16 = mybir.dt.bfloat16
I32 = mybir.dt.int32
U32 = mybir.dt.uint32
U16 = mybir.dt.uint16
U8 = mybir.dt.uint8
FP8X4 = mybir.dt.float8_e4m3fn_x4
FP4X4 = mybir.dt.float4_e2m1fn_x4
ALU = mybir.AluOpType
COPY = mybir.ActivationFunctionType.Copy

P = 128
PACK = 4
LAST = PACK - 1
HALF = S // 2
QUARTER = S // 4
D = 3
PER_COLUMN = 16
QUADRANT = 32
UNIT = 256


def tile_picked_huber_none_e_kernel(
    tc, xT, w1_words, w1_scales, bound, offs, cen, pos1, pos2, pos3, out
):
    nc = tc.nc
    with ExitStack() as ctx:
        keep = ctx.enter_context(tc.tile_pool(name="keep", bufs=1))
        psum = ctx.enter_context(tc.psum_pool(name="psum", bufs=1))

        def sbuf(name, shape, dtype=F32, over=None):
            return keep.tile([P] + shape, dtype, name=name, tag=over or name, align_bytes=64)

        def load_list(src, name):
            tile = keep.tile(list(src.shape), U16, name=name)
            nc.sync.dma_start(tile[:], src)
            return tile

        def entries(list_tile, first, count):
            return list_tile[:, first // PER_COLUMN : (first + count) // PER_COLUMN]

        def bank_tile(name, width, bank):
            return psum.tile([P, width], F32, name=name, tag=f"bank{bank}")

        def part(ap, i, width=P):
            return ap[:, i * width : (i + 1) * width]

        w_scales = sbuf("w_scales", [N], U8)
        nc.vector.memset(w_scales[:].bitcast(I32), 0)
        ident = sbuf("ident", [P])
        make_identity(nc, ident[:])

        rows = xT.rearrange("(p t) c -> p t c", t=PACK)
        planes = [sbuf(f"plane{t}", [T]) for t in range(PACK)]
        nc.sync.dma_start(planes[0][:], rows[:, 0, :])
        offs_sb = load_list(offs, "offs_sb")
        for t in range(1, PACK):
            nc.sync.dma_start(planes[t][:], rows[:, t, :])
        for q in range(P // QUADRANT):
            nc.sync.dma_start(
                w_scales[QUADRANT * q : QUADRANT * q + 4, :].bitcast(I32),
                w1_scales[0, 4 * q : 4 * q + 4, :].bitcast(I32),
            )
        far = sbuf("far", [UNIT])
        nc.sync.dma_start(far[:], bound[:, V - UNIT :])
        cen_sb = load_list(cen, "cen_sb")
        w_words = sbuf("w_words", [2 * N], U8)
        nc.sync.dma_start(w_words[:], w1_words[0])
        pos_sb = [load_list(src, f"pos{d}_sb") for d, src in enumerate((pos1, pos2, pos3))]
        upper = sbuf("upper", [V // P])
        with nc.allow_non_contiguous_dma(reason="512 bounds, one target a partition"):
            nc.sync.dma_start(upper[:], bound[0].rearrange("(c p) -> p c", p=P))

        first_half = sbuf("first_half", [HALF, PACK], BF16)
        quarters = [sbuf(f"quarter{i}", [QUARTER, PACK], BF16) for i in range(2)]

        def fetch(name, t, first, count):
            tile = sbuf(name, [count], BF16)
            nc.scalar.activation(tile[:], planes[t][:].indirect(entries(offs_sb, first, count)), COPY)
            return tile

        for t in range(PACK):
            nc.vector.tensor_copy(first_half[:, :, t], planes[t][:].indirect(entries(offs_sb, 0, HALF)))
            if t < LAST:
                plain = fetch(f"plain{t}", t, HALF, HALF)
                for i in range(2):
                    nc.scalar.copy(quarters[i][:, :, t], part(plain, i, QUARTER))
        eighth = fetch("last0", LAST, HALF, P)
        others = fetch("last1", LAST, HALF + P, HALF - P)
        nc.vector.tensor_copy(quarters[0][:, :P, LAST], eighth[:])
        nc.scalar.copy(quarters[0][:, P:, LAST], others[:, :P])
        nc.scalar.copy(quarters[1][:, :, LAST], others[:, P:])

        codes = [sbuf("codes0", [HALF], U32, over=f"plane{LAST}"), sbuf("codes1", [HALF], U32)]
        scales = [sbuf(f"scales{h}", [HALF], U8) for h in range(2)]
        y = [sbuf(f"y{b}", [S]) for b in range(N // P)]

        def product(b, h, cols, bank):
            acc = bank_tile("acc", cols.stop - cols.start, bank)
            nc.tensor.matmul_mx(
                out=acc[:],
                lhsT=w_words[:, 2 * P * b : 2 * P * (b + 1)].bitcast(FP4X4),
                lhsT_scale=part(w_scales, b),
                rhs=codes[h][:, cols].bitcast(FP8X4),
                rhs_scale=scales[h][:, cols],
                start=True,
                stop=True,
            )
            return acc

        def bring_out(b, h, cols, acc, engine):
            dst = y[b][:, h * HALF + cols.start : h * HALF + cols.stop]
            if engine == "vector":
                nc.vector.tensor_copy(dst, acc[:])
            else:
                nc.scalar.copy(dst, acc[:])

        steps = [
            (0, 0, first_half[:, :QUARTER, :], "scalar"),
            (0, QUARTER, first_half[:, QUARTER:, :], "scalar"),
            (1, 0, quarters[0][:], "vector"),
            (1, QUARTER, quarters[1][:, :P, :], "scalar"),
            (1, QUARTER + P, quarters[1][:, P:, :], "vector"),
        ]
        for bank, (h, first, src, engine) in enumerate(steps):
            cols = slice(first, first + src.shape[1])
            nc.vector.quantize_mx(
                out=codes[h][:, cols].bitcast(FP8X4),
                scales=scales[h][:, cols],
                in_=src.rearrange("p j t -> p (j t)"),
            )
            bring_out(0, h, cols, product(0, h, cols, bank), engine)
            if bank == 1:
                early = slice(0, QUARTER)
                bring_out(1, 0, early, product(1, 0, early, 7), "scalar")
        later = [slice(QUARTER, HALF), slice(0, HALF)]
        second = [product(1, h, later[h], 2 + h) for h in range(2)]

        reach = sbuf("reach", [UNIT], over="quarter1")
        nc.gpsimd.tensor_scalar(reach[:], far[:], 1.0 / D, 0.0, ALU.mult, ALU.add)

        def picked_by(list_tile, b, first, count=UNIT):
            return y[b][:].indirect(entries(list_tile, first, count))

        def fetch_scalar(name, list_tile, b, first, count=UNIT, scale=1.0):
            dst = sbuf(name, [count])
            nc.scalar.activation(dst[:], picked_by(list_tile, b, first, count), COPY, scale=scale)
            return dst

        def group(name, width, bank, count):
            return {"tile": bank_tile(name, width, bank), "left": count, "count": count}

        def turn(g, slot, src):
            g["left"] -= 1
            nc.tensor.matmul(
                part(g["tile"], slot), src, ident[:],
                start=g["left"] == g["count"] - 1, stop=g["left"] == 0, is_transpose=True,
            )

        def clip(name, chunk, source):
            dst = sbuf(name, [source.shape[1]])
            col = slice(chunk, chunk + 1)
            nc.vector.tensor_scalar(dst[:], source, upper[:, col], lower[:, col], ALU.min, ALU.max)
            return dst

        def turn_back(g, slot, clipped):
            for d in range(clipped.shape[1] // P):
                turn(g, slot, part(clipped, d))

        def mean(dst, sums, negated):
            nc.vector.scalar_tensor_tensor(dst, sums, 1.0 / D, negated, ALU.mult, ALU.subtract)

        t0 = [group(f"t0_{c}", D * P, c, D + 1) for c in range(2)]
        neg0 = fetch_scalar("neg0", cen_sb, 0, 0, scale=-1.0)
        pull = sbuf("pull00", [UNIT])
        nc.vector.tensor_copy(pull[:], picked_by(pos_sb[0], 0, 0))
        for c in range(2):
            turn(t0[c], 0, part(pull, c))
            turn(t0[c], 0, part(neg0, c))
        for d in range(1, D):
            pull = sbuf(f"pull0{d}", [UNIT])
            nc.vector.tensor_tensor(pull[:], picked_by(pos_sb[d], 0, 0), neg0[:], ALU.add)
            for c in range(2):
                turn(t0[c], d, part(pull, c))
        centre = fetch_scalar("centre", cen_sb, 0, UNIT, scale=1.0 / D)
        for h in range(2):
            bring_out(1, h, later[h], second[h], "scalar")
        near = sbuf("near", [D, UNIT], over="pull00")
        for d in range(D):
            nc.vector.tensor_copy(near[:, d, :], picked_by(pos_sb[d], 0, UNIT))
        limits = sbuf("limits", [2 * UNIT + V // P], over="pull01")
        high, low, lower = part(limits, 0, UNIT), part(limits, 1, UNIT), limits[:, 2 * UNIT :]
        nc.gpsimd.tensor_scalar(lower, upper[:], -1.0, 0.0, ALU.mult, ALU.add)
        nc.gpsimd.tensor_tensor(high, centre[:], reach[:], ALU.add)
        nc.gpsimd.tensor_tensor(low, centre[:], reach[:], ALU.subtract)

        neg2 = fetch_scalar("neg2", cen_sb, 1, 0, scale=-1.0)
        neg3 = fetch_scalar("neg3", cen_sb, 1, UNIT, scale=-1.0)
        t2 = [group("t2_0", (D + 1) * P, 5, 3 * D), group("t2_1", D * P, 6, 2 * D)]
        thirds = group("thirds", 3 * P, 4, 4 + D)
        for c in range(2):
            for d in range(D):
                turn(t2[c], d, part(neg2, c))
        for c in range(2):
            turn(thirds, c, part(neg3, c))
        pairs = [group("pair0", D * P, 2, 4 + D)]
        for d in range(2):
            turn(pairs[0], d, part(neg3, 0))
        pulls2 = [fetch_scalar(f"pull2{d}", pos_sb[d], 1, 0) for d in range(D)]
        pulls3 = [fetch_scalar(f"pull3{d}", pos_sb[d], 1, UNIT) for d in range(2)]
        pieces = [fetch_scalar(f"piece{c}", pos_sb[2], 1, UNIT + c * P, P) for c in range(2)]
        for c in range(2):
            turn(t2[c], 0, part(pulls2[0], c))
        turn_back(t2[0], D, clip("clipped0", 0, t0[0]["tile"][:]))
        for d in range(1, D):
            for c in range(2):
                turn(t2[c], d, part(pulls2[d], c))

        def thrice(ap):
            return ap.unsqueeze(1).to_broadcast([P, D, UNIT])

        below = sbuf("below", [D, UNIT], over="pull02")
        nc.vector.scalar_tensor_tensor(below[:], near[:], 1.0 / D, thrice(high), ALU.mult, ALU.min)
        turn_back(pairs[0], 2, clip("clipped1", 1, t0[1]["tile"][:]))
        pairs.append(group("pair1", 2 * P, 1, 4))
        for d in range(2):
            turn(pairs[1], d, part(neg3, 1))
        for d in range(2):
            for c in range(2):
                turn(pairs[c], d, part(pulls3[d], c))
        inside = sbuf("inside", [D, UNIT])
        nc.vector.tensor_tensor(inside[:], below[:], thrice(low), ALU.max)
        turn_back(thirds, 2, clip("clipped4", 0, t2[0]["tile"][:, : D * P]))
        for c in range(2):
            turn(thirds, c, pieces[c][:])
        two = sbuf("two", [UNIT])
        result1 = sbuf("result1", [UNIT])
        nc.gpsimd.tensor_tensor(two[:], inside[:, 0, :], inside[:, 1, :], ALU.add)
        nc.gpsimd.tensor_tensor(result1[:], two[:], inside[:, 2, :], ALU.add)
        for c in range(2):
            nc.sync.dma_start(out[:P, UNIT + c * P : UNIT + (c + 1) * P], part(result1, c))
        sum2b = group("sum2b", P, 7, D)
        turn_back(sum2b, 0, clip("clipped5", 1, t2[1]["tile"][:, : D * P]))
        sum3 = [group(f"sum3_{c}", P, 3 * c, D) for c in range(2)]
        for c in range(2):
            turn_back(sum3[c], 0, clip(f"pair{c}", 2 + c, pairs[c]["tile"][:, :UNIT]))
        moved = sbuf("moved", [UNIT])
        for c, sums in enumerate((part(t2[0]["tile"], D), part(pairs[0]["tile"], 2))):
            nc.scalar.activation(part(moved, c), sums, COPY, scale=1.0 / D)
        result0 = sbuf("result0", [UNIT])
        nc.gpsimd.tensor_tensor(result0[:], moved[:], neg0[:], ALU.subtract)
        for c in range(2):
            nc.scalar.dma_start(out[:P, c * P : (c + 1) * P], part(result0, c))
        for c in range(2):
            turn_back(sum3[c], 0, clip(f"third{c}", 2 + c, part(thirds["tile"], c)))
        second_rows = sbuf("second_rows", [V])
        ends = [part(thirds["tile"], 2), sum2b["tile"][:], sum3[0]["tile"][:], sum3[1]["tile"][:]]
        for c, src in enumerate(ends):
            mean(part(second_rows, c), src, part((neg2, neg3)[c // 2], c % 2))
            nc.sync.dma_start(out[P:, c * P : (c + 1) * P], part(second_rows, c))
